import numpy as np
import ml_dtypes


def mxq(x, axis, fmt="e4m3"):
    dtype, down = {"e4m3": (ml_dtypes.float8_e4m3fn, 7), "e5m2": (ml_dtypes.float8_e5m2, 14)}[fmt]
    v = np.moveaxis(np.asarray(x, np.float32).astype(ml_dtypes.bfloat16).astype(np.float64), axis, -1)
    blocks = v.reshape(v.shape[:-1] + (-1, 32))
    amax = np.abs(blocks).max(-1, keepdims=True)
    byte = np.maximum(np.where(amax > 0, np.frexp(amax)[1] - 1 + 127, 0) - down, 1)
    scale = np.exp2(byte - 127.0)
    codes = (blocks / scale).astype(np.float32).astype(dtype).astype(np.float64)
    return np.moveaxis((codes * scale).reshape(v.shape), -1, axis)


WIDE = False


def mx_kscale(k):
    if not WIDE:
        return np.ones(k)
    levels = np.array([30, -30])
    if k % 512:
        return np.exp2(np.random.permutation(np.resize(levels, k // 32))).repeat(32)
    a = np.empty((k // 512, 16))
    for p in range(k // 512):
        a[p, :8] = np.random.permutation(np.resize(levels, 8))
        for g in range(8):
            far = levels[np.abs(levels - a[p, g]) >= 10]
            a[p, g + 8] = far[np.random.randint(len(far))]
    return np.exp2(a.ravel()).repeat(32)


BF16 = ml_dtypes.bfloat16


def bf(x):
    return np.asarray(x, np.float32).astype(BF16)


def f64(x):
    return np.asarray(x).astype(np.float64)


E2M1 = np.array([0.0, 0.5, 1.0, 1.5, 2.0, 3.0, 4.0, 6.0, -0.0, -0.5, -1.0, -1.5, -2.0, -3.0, -4.0, -6.0])


def pack_weight(w, fmt):
    k, n = w.shape
    w = f64(bf(w)).reshape(k // 32, 32, n)
    amax = np.abs(w).max(1)
    if fmt == "e4m3":
        byte = np.frexp(amax)[1] - 1 + 127 - 7
    else:
        mant, ex = np.frexp(amax / 6.0)
        byte = np.where(mant > 0.5, ex, ex - 1) + 127
    byte = np.clip(np.where(amax > 0, byte, 1), 1, 254)
    scaled = (w * np.exp2(127.0 - byte)[:, None, :]).reshape(k, n).astype(np.float32)
    by_word = np.ascontiguousarray(scaled.reshape(k // 512, 128, 4, n).transpose(0, 1, 3, 2))
    if fmt == "e4m3":
        words = by_word.astype(ml_dtypes.float8_e4m3fn).view(np.uint8)
    else:
        c = by_word.astype(ml_dtypes.float4_e2m1fn).view(np.uint8) & 0xF
        words = c[..., 0::2] | (c[..., 1::2] << 4)
    return np.ascontiguousarray(words), np.ascontiguousarray(byte.astype(np.uint8).reshape(k // 512, 16, n))


def unpack_weight(words, scales, fmt):
    g, p, n, _ = words.shape
    if fmt == "e4m3":
        vals = np.ascontiguousarray(words).view(ml_dtypes.float8_e4m3fn).astype(np.float64)
    else:
        nib = np.empty((g, p, n, 4), np.uint8)
        nib[..., 0::2] = words & 0xF
        nib[..., 1::2] = words >> 4
        vals = E2M1[nib]
    vals = vals * np.repeat(np.exp2(scales.astype(np.float64) - 127.0), 8, axis=1)[..., None]
    return vals.transpose(0, 1, 3, 2).reshape(g * 512, n)
def pack4(w):
    words, scales = pack_weight(w, "e2m1")
    return words.reshape(words.shape[0], 128, -1), scales


def unpack4(words, scales):
    return unpack_weight(words.reshape(words.shape[0], 128, -1, 2), scales, "e2m1")


B, X, Y = 512, 1024, 1536
SPREAD, POPULAR, PEAK, CAP, BETA = 1.25, 0.3, 2.0, 3.0, 16.0


def setup_inputs():
    s, t = mx_kscale(X), mx_kscale(Y)
    chan = np.exp(SPREAD * np.random.standard_normal((X, Y)) + POPULAR * np.random.standard_normal(Y))
    chan = chan * Y / chan.sum(axis=1, keepdims=True)
    prior = np.exp(PEAK * np.clip(np.random.standard_normal((B, X)), -CAP, CAP))
    prior = prior / prior.sum(axis=1, keepdims=True)
    chan_words, chan_scales = pack4(chan / s[:, None])
    return {"prior": bf(prior * s),
            "chan_words": chan_words,
            "chan_scales": chan_scales,
            "beta": bf(BETA * (1 + 0.1 * np.random.standard_normal(Y)) * t),
            "channel_t": bf(chan.T / Y / t[:, None]),
            "score": bf(0.5 * np.random.standard_normal(X)),
            "anchor": bf(np.exp(0.5 * np.random.standard_normal((B, X))))}


def reference(prior, chan_words, chan_scales, beta, channel_t, score, anchor):
    o = mxq(f64(prior), 1, "e4m3") @ unpack4(chan_words, chan_scales)
    l = f64(beta) * np.log(o)
    c = mxq(l, 1, "e5m2") @ mxq(f64(channel_t), 0, "e4m3")
    return f64(anchor) * np.exp(f64(score) - c)

@@ -1,0 +1,362 @@
+from contextlib import ExitStack
+
+import concourse.mybir as mybir
+from concourse.masks import make_identity
+
+B, X, Y = 512, 1024, 1536
+FLOPS = 2 * B * X * Y * 2
+
+F32 = mybir.dt.float32
+BF16 = mybir.dt.bfloat16
+I32 = mybir.dt.int32
+U32 = mybir.dt.uint32
+U8 = mybir.dt.uint8
+E4M3 = mybir.dt.float8_e4m3fn_x4
+E5M2 = mybir.dt.float8_e5m2_x4
+E2M1 = mybir.dt.float4_e2m1fn_x4
+ACT = mybir.ActivationFunctionType
+MULT = mybir.AluOpType.mult
+
+P = 128
+KX = X // 512
+GY = Y // 512
+XT = X // P
+
+
+def tile_anchored_log_output_reweighting_s9_kernel(tc, prior, chan_words, chan_scales, beta, channel_t, score, anchor, out):
+    nc = tc.nc
+    with ExitStack() as ctx:
+        keep = ctx.enter_context(tc.tile_pool(name="keep", bufs=1))
+        acc_pool = ctx.enter_context(tc.psum_pool(name="acc_pool", bufs=6))
+        tp_pool = ctx.enter_context(tc.psum_pool(name="tp_pool", bufs=2))
+
+        def sb(shape, dtype, name):
+            return keep.tile(shape, dtype, name=name, align_bytes=64)
+
+        ident = sb([P, P], F32, "ident")
+        ident_bf = sb([P, P], BF16, "ident_bf")
+        warm = sb([P, 2], F32, "warm")
+        p_raw = [sb([P, 4, 512], BF16, f"p_raw{k}") for k in range(KX)]
+        p_grp = [sb([P, 512, 4], BF16, f"p_grp{k}") for k in range(KX)]
+        p_code = [sb([P, 512], U32, f"p_code{k}") for k in range(KX)]
+        p_scale = [sb([P, 512], U8, f"p_scale{k}") for k in range(KX)]
+        w_raw = [sb([P, KX, 1024], U8, f"w_raw{g}") for g in range(GY)]
+        w_code = [sb([P, KX, 1024], U8, f"w_code{g}") for g in range(GY)]
+        ws_raw = sb([P, KX, Y], U8, "ws_raw")
+        w_scale = sb([P, KX, Y], U8, "w_scale")
+        vec_rows = sb([P, GY, P], BF16, "vec_rows")
+        vec_cols = sb([P, GY, 12], F32, "vec_cols")
+        ln_o = [sb([P, 4, 512], F32, f"ln_o{g}") for g in range(GY)]
+        l_grp = [sb([P, 512, 4], BF16, f"l_grp{g}") for g in range(GY)]
+        l_code = [sb([P, 512], U32, f"l_code{g}") for g in range(GY)]
+        l_scale = [sb([P, 512], U8, f"l_scale{g}") for g in range(GY)]
+        c_raw = [sb([P, 4, X], BF16, f"c_raw{g}") for g in range(GY)]
+        c_grp = [sb([P, X, 4], BF16, f"c_grp{g}") for g in range(GY)]
+        c_code = [sb([P, X], U32, f"c_code{g}") for g in range(GY)]
+        c_scale = [sb([P, X], U8, f"c_scale{g}") for g in range(GY)]
+        anc = sb([P, 4, X], BF16, "anc")
+        e_x = [sb([P, 512], F32, f"e_x{i}") for i in range(XT)]
+        o_sb = [sb([P, 4, 256], F32, f"o_sb{i}") for i in range(XT // 2 - 1)]
+        o_last = [sb([P, 4, P], F32, f"o_last{i}") for i in range(2)]
+
+        prior_v = prior.rearrange("(j p) x -> p j x", p=P)
+        anchor_v = anchor.rearrange("(j p) x -> p j x", p=P)
+        out_v = out.rearrange("(j p) x -> p j x", p=P)
+        acc = {}
+        tps = {}
+
+        def load_prior(k, j0, j1):
+            nc.sync.dma_start(out=p_raw[k][:, j0:j1, :], in_=prior_v[:, j0:j1, 512 * k : 512 * k + 512])
+
+        def load_w(g):
+            src = chan_words[:, :, 1024 * g : 1024 * g + 1024].bitcast(I32)
+            nc.sync.dma_start(out=w_raw[g][:].bitcast(I32), in_=src.rearrange("k p n -> p k n"))
+
+        def load_c(g, x0, x1):
+            rows = channel_t[512 * g : 512 * g + 512, x0:x1].rearrange("(a t e) x -> e a t x", t=4, e=4)
+            for e in range(4):
+                nc.sync.dma_start(out=c_raw[g][e:P:4, :, x0:x1], in_=rows[e])
+
+        def turn_prior(k, h):
+            tp = acc_pool.tile([P, 2, 2, P], F32, name="acc")
+            tps["p", k, h] = tp
+            words = p_raw[k][:].bitcast(F32)
+            for j in range(2):
+                for u in range(2):
+                    nc.tensor.transpose(tp[:, j, u, :], words[:, 2 * h + j, u:256:2], ident[:])
+
+        def copy_prior(k, h, copy):
+            dst = p_grp[k][:, 256 * h : 256 * h + 256, :].bitcast(F32).rearrange("p (j b) u -> p j b u", j=2)
+            copy(out=dst, in_=tps["p", k, h][:].rearrange("p j u b -> p j b u"))
+
+        def quant_prior(k, h):
+            b = slice(256 * h, 256 * h + 256)
+            nc.vector.quantize_mx(out=p_code[k][:, b].bitcast(E4M3), scales=p_scale[k][:, b], in_=p_grp[k][:, b, :].rearrange("p b t -> p (b t)"))
+
+        def permute_w1(g, k):
+            nc.vector.tensor_copy(
+                out=w_code[g][:, k, :].bitcast(I32).rearrange("p (t a w) -> p t a w", t=4, w=2),
+                in_=w_raw[g][:, k, :].bitcast(I32).rearrange("p (a t w) -> p t a w", t=4, w=2),
+            )
+
+        def permute_ws():
+            nc.vector.tensor_copy(
+                out=w_scale[:].bitcast(I32).rearrange("p k (t a) -> p k t a", t=4),
+                in_=ws_raw[:].bitcast(I32).rearrange("p k (a t) -> p k t a", t=4),
+            )
+
+        def mm1(n, k):
+            g, t = divmod(n, 4)
+            if k == 0:
+                acc["o", n] = acc_pool.tile([P, 512], F32, name="acc")
+            col = (t * GY + g) * P
+            nc.tensor.matmul_mx(
+                out=acc["o", n][:],
+                lhsT=w_code[g][:, k, 256 * t : 256 * t + 256].bitcast(E2M1),
+                lhsT_scale=w_scale[:, k, col : col + P],
+                rhs=p_code[k][:].bitcast(E4M3),
+                rhs_scale=p_scale[k][:],
+                start=(k == 0),
+                stop=(k == KX - 1),
+            )
+
+        def log_o(n):
+            g, t = divmod(n, 4)
+            nc.scalar.activation(out=ln_o[g][:, t, :], in_=acc["o", n][:], func=ACT.Ln)
+
+        def beta_mul(g):
+            b_row = vec_cols[:, g, 0:4].unsqueeze(1).unsqueeze(3).to_broadcast([P, 128, 4, 4])
+            nc.vector.tensor_tensor(
+                out=l_grp[g][:].rearrange("p (c i) t -> p c t i", i=4),
+                in0=ln_o[g][:].rearrange("p t (c i) -> p c t i", i=4),
+                in1=b_row,
+                op=MULT,
+            )
+
+        def quant_l(g):
+            nc.vector.quantize_mx(out=l_code[g][:].bitcast(E5M2), scales=l_scale[g][:], in_=l_grp[g][:].rearrange("p b t -> p (b t)"))
+
+        def group_c(g, q, copy):
+            x0 = 256 * q
+            copy(
+                out=c_grp[g][:, x0 : x0 + 256, :].rearrange("p (c i) t -> p c t i", i=4),
+                in_=c_raw[g][:, :, x0 : x0 + 256].rearrange("p t (c i) -> p c t i", i=4),
+            )
+
+        def quant_c(g, x0, x1):
+            nc.vector.quantize_mx(
+                out=c_code[g][:, x0:x1].bitcast(E4M3),
+                scales=c_scale[g][:, x0:x1],
+                in_=c_grp[g][:, x0:x1, :].rearrange("p x t -> p (x t)"),
+            )
+
+        def mm2(x, g):
+            if g == 0:
+                acc["c", x] = acc_pool.tile([P, 512], F32, name="acc")
+            col = slice(P * x, P * x + P)
+            nc.tensor.matmul_mx(
+                out=acc["c", x][:],
+                lhsT=c_code[g][:, col].bitcast(E4M3),
+                lhsT_scale=c_scale[g][:, col],
+                rhs=l_code[g][:].bitcast(E5M2),
+                rhs_scale=l_scale[g][:],
+                start=(g == 0),
+                stop=(g == GY - 1),
+            )
+
+        def exp_c(x):
+            nc.scalar.activation(out=e_x[x][:], in_=acc["c", x][:], func=ACT.Exp, scale=-1.0, bias=vec_cols[:, 0, 4 + x : 5 + x])
+
+        def turn_e(x):
+            tp = tp_pool.tile([P, 4, P], F32, name="tp")
+            tps["e", x] = tp
+            for j in range(4):
+                nc.tensor.transpose(tp[:, j, :], e_x[x][:, P * j : P * j + P], ident[:])
+
+        def anchor_mul(x):
+            half = P * (x % 2)
+            nc.vector.tensor_tensor(
+                out=o_sb[x // 2][:, :, half : half + P] if x < 6 else o_last[x - 6][:], in0=tps["e", x][:], in1=anc[:, :, P * x : P * x + P], op=MULT
+            )
+
+        def store(i):
+            nc.sync.dma_start(out=out_v[:, :, 256 * i : 256 * i + 256], in_=o_sb[i][:])
+
+        def store_x(x):
+            nc.sync.dma_start(out=out_v[:, :, P * x : P * x + P], in_=o_last[x - 6][:])
+
+        def scales_in(r):
+            nc.scalar.dma_start(
+                out=ws_raw[r:P:32, :, :].bitcast(I32),
+                in_=chan_scales[:, r:16:4, :].bitcast(I32).rearrange("k q y -> q k y"),
+            )
+
+        vcopy, scopy = nc.vector.tensor_copy, nc.scalar.copy
+
+        with tc.manual_schedule():
+            nc.vector.memset(ws_raw[:].rearrange("p k y -> p (k y)").bitcast(I32), 0)
+            nc.vector.memset(warm[:], 1.0)
+            nc.vector.memset(vec_rows[:], 0.0)
+            make_identity(nc, ident[:])
+            load_prior(0, 0, 4)
+            load_prior(1, 0, 2)
+            load_prior(1, 2, 4)
+            load_w(0)
+            for r in range(4):
+                scales_in(r)
+            nc.scalar.activation(out=warm[:, 1:2], in_=warm[:, 0:1], func=ACT.Ln)
+            nc.gpsimd.dma_start(
+                out=vec_rows[0:4, :, :].rearrange("t g (a e) -> t (g a) e", e=4), in_=beta.rearrange("(a t e) -> t a e", t=4, e=4)
+            )
+            nc.gpsimd.dma_start(out=vec_rows[4 : 4 + XT, 0, :], in_=score.rearrange("(r m) -> r m", m=P))
+            make_identity(nc, ident_bf[:])
+            load_c(0, 0, 1024)
+            load_w(1)
+            load_c(1, 0, 1024)
+            load_w(2)
+            load_c(2, 0, 1024)
+            for h in range(2):
+                nc.sync.dma_start(out=anc[:, :, 512 * h : 512 * h + 512], in_=anchor_v[:, :, 512 * h : 512 * h + 512])
+            turn_prior(0, 1)
+            copy_prior(0, 1, vcopy)
+            quant_prior(0, 1)
+            turn_prior(1, 0)
+            copy_prior(1, 0, scopy)
+            turn_prior(1, 1)
+            copy_prior(1, 1, scopy)
+            permute_ws()
+            permute_w1(0, 0)
+            turn_prior(0, 0)
+            copy_prior(0, 0, scopy)
+            group_c(0, 3, scopy)
+            quant_prior(0, 0)
+            mm1(2, 0)
+            quant_prior(1, 0)
+            quant_prior(1, 1)
+            permute_w1(0, 1)
+            vec_t = tp_pool.tile([P, GY, P], BF16, name="tp")
+            for g in range(GY):
+                nc.tensor.transpose(vec_t[:, g, :], vec_rows[:, g, :], ident_bf[:])
+            group_c(0, 2, vcopy)
+            mm1(0, 0)
+            mm1(0, 1)
+            permute_w1(1, 0)
+            mm1(2, 1)
+            group_c(0, 0, scopy)
+            mm1(1, 0)
+            mm1(5, 0)
+            mm1(1, 1)
+            group_c(0, 1, vcopy)
+            quant_c(0, 512, 768)
+            log_o(0)
+            vcopy(out=vec_cols[:], in_=vec_t[:, :, 0:12])
+            mm1(3, 0)
+            mm1(3, 1)
+            log_o(2)
+            quant_c(0, 768, 1024)
+            log_o(3)
+            quant_c(0, 0, 256)
+            mm1(7, 0)
+            quant_c(0, 256, 512)
+            permute_w1(1, 1)
+            mm1(5, 1)
+            log_o(1)
+            mm1(4, 0)
+            mm1(4, 1)
+            log_o(5)
+            group_c(1, 0, vcopy)
+            permute_w1(2, 0)
+            group_c(1, 1, vcopy)
+            group_c(1, 2, scopy)
+            mm1(6, 0)
+            mm1(6, 1)
+            log_o(6)
+            log_o(4)
+            beta_mul(0)
+            mm1(8, 0)
+            mm1(7, 1)
+            log_o(7)
+            permute_w1(2, 1)
+            mm1(9, 0)
+            mm1(9, 1)
+            mm1(8, 1)
+            log_o(8)
+            mm1(10, 0)
+            mm1(10, 1)
+            quant_c(1, 0, 256)
+            mm1(11, 0)
+            mm1(11, 1)
+            quant_l(0)
+            mm2(3, 0)
+            quant_c(1, 256, 512)
+            log_o(10)
+            beta_mul(1)
+            mm2(4, 0)
+            quant_c(1, 512, 768)
+            quant_l(1)
+            mm2(2, 0)
+            mm2(0, 0)
+            mm2(2, 1)
+            mm2(1, 0)
+            mm2(1, 1)
+            mm2(5, 0)
+            log_o(9)
+            log_o(11)
+            beta_mul(2)
+            group_c(2, 1, scopy)
+            group_c(2, 0, scopy)
+            group_c(2, 2, scopy)
+            mm2(5, 1)
+            mm2(4, 1)
+            nc.scalar.activation(out=warm[:, 1:2], in_=warm[:, 0:1], func=ACT.Exp)
+            quant_c(2, 256, 512)
+            mm2(3, 1)
+            quant_l(2)
+            mm2(0, 1)
+            mm2(3, 2)
+            quant_c(2, 0, 256)
+            exp_c(3)
+            mm2(2, 2)
+            mm2(0, 2)
+            mm2(1, 2)
+            exp_c(1)
+            quant_c(2, 512, 768)
+            mm2(4, 2)
+            turn_e(3)
+            group_c(1, 3, vcopy)
+            exp_c(0)
+            group_c(2, 3, vcopy)
+            turn_e(1)
+            anchor_mul(3)
+            anchor_mul(1)
+            turn_e(0)
+            anchor_mul(0)
+            store(0)
+            quant_c(1, 768, 1024)
+            exp_c(2)
+            turn_e(2)
+            mm2(5, 2)
+            anchor_mul(2)
+            store(1)
+            mm2(7, 0)
+            mm2(7, 1)
+            exp_c(4)
+            turn_e(4)
+            exp_c(5)
+            turn_e(5)
+            quant_c(2, 768, 1024)
+            mm2(7, 2)
+            anchor_mul(4)
+            exp_c(7)
+            mm2(6, 0)
+            mm2(6, 1)
+            mm2(6, 2)
+            anchor_mul(5)
+            store(2)
+            turn_e(7)
+            exp_c(6)
+            turn_e(6)
+            anchor_mul(7)
+            store_x(7)
+            anchor_mul(6)
+            store_x(6)

@@ -44,8 +44,10 @@ def tile_anchored_log_output_reweighting_s9_kernel(tc, prior, chan_words, chan_s
         w_code = [sb([P, KX, 1024], U8, f"w_code{g}") for g in range(GY)]
         ws_raw = sb([P, KX, Y], U8, "ws_raw")
         w_scale = sb([P, KX, Y], U8, "w_scale")
-        vec_rows = sb([P, GY, P], BF16, "vec_rows")
-        vec_cols = sb([P, GY, 12], F32, "vec_cols")
+        vec_rows = sb([P, 512], BF16, "vec_rows")
+        vec_perm = sb([P, 512], BF16, "vec_perm")
+        beta_cols = sb([P, GY, 4], F32, "beta_cols")
+        score_cols = sb([P, XT], F32, "score_cols")
         ln_o = [sb([P, 4, 512], F32, f"ln_o{g}") for g in range(GY)]
         l_grp = [sb([P, 512, 4], BF16, f"l_grp{g}") for g in range(GY)]
         l_code = [sb([P, 512], U32, f"l_code{g}") for g in range(GY)]
@@ -125,7 +127,7 @@ def tile_anchored_log_output_reweighting_s9_kernel(tc, prior, chan_words, chan_s
             nc.scalar.activation(out=ln_o[g][:, t, :], in_=acc["o", n][:], func=ACT.Ln)
 
         def beta_mul(g):
-            b_row = vec_cols[:, g, 0:4].unsqueeze(1).unsqueeze(3).to_broadcast([P, 128, 4, 4])
+            b_row = beta_cols[:, g, :].unsqueeze(1).unsqueeze(3).to_broadcast([P, 128, 4, 4])
             nc.vector.tensor_tensor(
                 out=l_grp[g][:].rearrange("p (c i) t -> p c t i", i=4),
                 in0=ln_o[g][:].rearrange("p t (c i) -> p c t i", i=4),
@@ -165,7 +167,7 @@ def tile_anchored_log_output_reweighting_s9_kernel(tc, prior, chan_words, chan_s
             )
 
         def exp_c(x):
-            nc.scalar.activation(out=e_x[x][:], in_=acc["c", x][:], func=ACT.Exp, scale=-1.0, bias=vec_cols[:, 0, 4 + x : 5 + x])
+            nc.scalar.activation(out=e_x[x][:], in_=acc["c", x][:], func=ACT.Exp, scale=-1.0, bias=score_cols[:, x : x + 1])
 
         def turn_e(x):
             tp = tp_pool.tile([P, 4, P], F32, name="tp")
@@ -186,7 +188,7 @@ def tile_anchored_log_output_reweighting_s9_kernel(tc, prior, chan_words, chan_s
             nc.sync.dma_start(out=out_v[:, :, P * x : P * x + P], in_=o_last[x - 6][:])
 
         def scales_in(r):
-            nc.scalar.dma_start(
+            nc.sync.dma_start(
                 out=ws_raw[r:P:32, :, :].bitcast(I32),
                 in_=chan_scales[:, r:16:4, :].bitcast(I32).rearrange("k q y -> q k y"),
             )
@@ -199,18 +201,17 @@ def tile_anchored_log_output_reweighting_s9_kernel(tc, prior, chan_words, chan_s
             nc.vector.memset(vec_rows[:], 0.0)
             make_identity(nc, ident[:])
             load_prior(0, 0, 4)
-            load_prior(1, 0, 2)
-            load_prior(1, 2, 4)
-            load_w(0)
             for r in range(4):
                 scales_in(r)
+            load_prior(1, 0, 2)
+            load_prior(1, 2, 4)
             nc.scalar.activation(out=warm[:, 1:2], in_=warm[:, 0:1], func=ACT.Ln)
-            nc.gpsimd.dma_start(
-                out=vec_rows[0:4, :, :].rearrange("t g (a e) -> t (g a) e", e=4), in_=beta.rearrange("(a t e) -> t a e", t=4, e=4)
-            )
-            nc.gpsimd.dma_start(out=vec_rows[4 : 4 + XT, 0, :], in_=score.rearrange("(r m) -> r m", m=P))
+            nc.gpsimd.dma_start(out=vec_rows[0:GY, :], in_=beta.rearrange("(g n) -> g n", g=GY))
+            nc.gpsimd.dma_start(out=vec_rows[4 : 4 + XT, 0:P], in_=score.rearrange("(r m) -> r m", m=P))
             make_identity(nc, ident_bf[:])
-            load_c(0, 0, 1024)
+            load_w(0)
+            load_c(0, 0, 512)
+            load_c(0, 512, 1024)
             load_w(1)
             load_c(1, 0, 1024)
             load_w(2)
@@ -218,145 +219,151 @@ def tile_anchored_log_output_reweighting_s9_kernel(tc, prior, chan_words, chan_s
             for h in range(2):
                 nc.sync.dma_start(out=anc[:, :, 512 * h : 512 * h + 512], in_=anchor_v[:, :, 512 * h : 512 * h + 512])
             turn_prior(0, 1)
-            copy_prior(0, 1, vcopy)
-            quant_prior(0, 1)
-            turn_prior(1, 0)
-            copy_prior(1, 0, scopy)
+            turn_prior(0, 0)
             turn_prior(1, 1)
-            copy_prior(1, 1, scopy)
+            copy_prior(0, 1, vcopy)
+            copy_prior(0, 0, vcopy)
+            quant_prior(0, 0)
             permute_ws()
             permute_w1(0, 0)
-            turn_prior(0, 0)
-            copy_prior(0, 0, scopy)
-            group_c(0, 3, scopy)
-            quant_prior(0, 0)
-            mm1(2, 0)
-            quant_prior(1, 0)
+            turn_prior(1, 0)
+            vcopy(
+                out=vec_perm[:].rearrange("p (t a e) -> p t a e", t=4, e=4),
+                in_=vec_rows[:].rearrange("p (a t e) -> p t a e", t=4, e=4),
+            )
+            quant_prior(0, 1)
+            mm1(1, 0)
+            copy_prior(1, 1, scopy)
             quant_prior(1, 1)
             permute_w1(0, 1)
-            vec_t = tp_pool.tile([P, GY, P], BF16, name="tp")
-            for g in range(GY):
-                nc.tensor.transpose(vec_t[:, g, :], vec_rows[:, g, :], ident_bf[:])
-            group_c(0, 2, vcopy)
+            group_c(0, 1, vcopy)
+            copy_prior(1, 0, scopy)
+            quant_prior(1, 0)
+            mm1(2, 0)
+            mm1(3, 0)
+            group_c(0, 0, scopy)
+            mm1(3, 1)
+            mm1(1, 1)
             mm1(0, 0)
             mm1(0, 1)
-            permute_w1(1, 0)
-            mm1(2, 1)
-            group_c(0, 0, scopy)
-            mm1(1, 0)
-            mm1(5, 0)
-            mm1(1, 1)
-            group_c(0, 1, vcopy)
-            quant_c(0, 512, 768)
-            log_o(0)
-            vcopy(out=vec_cols[:], in_=vec_t[:, :, 0:12])
-            mm1(3, 0)
-            mm1(3, 1)
-            log_o(2)
-            quant_c(0, 768, 1024)
-            log_o(3)
-            quant_c(0, 0, 256)
-            mm1(7, 0)
             quant_c(0, 256, 512)
-            permute_w1(1, 1)
-            mm1(5, 1)
-            log_o(1)
+            group_c(0, 2, vcopy)
+            permute_w1(1, 0)
+            quant_c(0, 512, 768)
+            mm1(2, 1)
+            vec_t = tp_pool.tile([P, 5, P], BF16, name="tp")
+            for t in range(4):
+                nc.tensor.transpose(vec_t[:, t, :], vec_perm[:, P * t : P * t + P], ident_bf[:])
+            nc.tensor.transpose(vec_t[:, 4, :], vec_rows[:, 0:P], ident_bf[:])
             mm1(4, 0)
+            group_c(0, 3, vcopy)
+            permute_w1(1, 1)
+            vcopy(out=beta_cols[:], in_=vec_t[:, 0:4, 0:GY].rearrange("p t g -> p g t"))
+            vcopy(out=score_cols[:], in_=vec_t[:, 4, 4 : 4 + XT])
             mm1(4, 1)
-            log_o(5)
+            mm1(7, 0)
+            log_o(1)
+            mm1(7, 1)
+            quant_c(0, 0, 256)
+            mm1(6, 0)
+            log_o(0)
             group_c(1, 0, vcopy)
             permute_w1(2, 0)
-            group_c(1, 1, vcopy)
-            group_c(1, 2, scopy)
-            mm1(6, 0)
-            mm1(6, 1)
-            log_o(6)
-            log_o(4)
-            beta_mul(0)
-            mm1(8, 0)
-            mm1(7, 1)
-            log_o(7)
-            permute_w1(2, 1)
-            mm1(9, 0)
-            mm1(9, 1)
-            mm1(8, 1)
-            log_o(8)
             mm1(10, 0)
+            log_o(3)
+            log_o(2)
+            group_c(1, 1, scopy)
+            log_o(4)
+            mm1(5, 0)
+            mm1(5, 1)
+            group_c(1, 2, vcopy)
+            mm1(11, 0)
+            log_o(5)
+            permute_w1(2, 1)
+            mm1(6, 1)
+            mm1(8, 0)
+            mm1(8, 1)
+            mm1(11, 1)
             mm1(10, 1)
             quant_c(1, 0, 256)
-            mm1(11, 0)
-            mm1(11, 1)
-            quant_l(0)
-            mm2(3, 0)
+            log_o(7)
+            mm1(9, 0)
+            mm1(9, 1)
+            log_o(6)
+            quant_c(1, 512, 768)
             quant_c(1, 256, 512)
+            beta_mul(0)
+            log_o(8)
+            group_c(2, 0, scopy)
+            log_o(11)
             log_o(10)
             beta_mul(1)
-            mm2(4, 0)
-            quant_c(1, 512, 768)
+            quant_l(0)
             quant_l(1)
             mm2(2, 0)
             mm2(0, 0)
-            mm2(2, 1)
-            mm2(1, 0)
-            mm2(1, 1)
-            mm2(5, 0)
-            log_o(9)
-            log_o(11)
-            beta_mul(2)
-            group_c(2, 1, scopy)
-            group_c(2, 0, scopy)
-            group_c(2, 2, scopy)
-            mm2(5, 1)
-            mm2(4, 1)
-            nc.scalar.activation(out=warm[:, 1:2], in_=warm[:, 0:1], func=ACT.Exp)
-            quant_c(2, 256, 512)
-            mm2(3, 1)
-            quant_l(2)
             mm2(0, 1)
-            mm2(3, 2)
+            mm2(4, 0)
+            log_o(9)
+            mm2(4, 1)
+            beta_mul(2)
+            mm2(5, 0)
+            mm2(3, 0)
+            mm2(1, 0)
+            group_c(2, 1, scopy)
+            quant_c(2, 256, 512)
+            mm2(2, 1)
+            mm2(3, 1)
+            nc.scalar.activation(out=warm[:, 1:2], in_=warm[:, 0:1], func=ACT.Exp)
+            mm2(5, 1)
+            group_c(2, 3, scopy)
+            mm2(1, 1)
+            quant_l(2)
             quant_c(2, 0, 256)
-            exp_c(3)
+            mm2(3, 2)
             mm2(2, 2)
+            exp_c(3)
+            group_c(2, 2, vcopy)
             mm2(0, 2)
-            mm2(1, 2)
-            exp_c(1)
-            quant_c(2, 512, 768)
-            mm2(4, 2)
-            turn_e(3)
             group_c(1, 3, vcopy)
+            mm2(1, 2)
+            turn_e(3)
+            quant_c(2, 512, 768)
             exp_c(0)
-            group_c(2, 3, vcopy)
+            turn_e(0)
+            exp_c(2)
+            mm2(5, 2)
+            turn_e(2)
+            mm2(4, 2)
+            exp_c(1)
             turn_e(1)
             anchor_mul(3)
-            anchor_mul(1)
-            turn_e(0)
+            quant_c(0, 768, 1024)
             anchor_mul(0)
-            store(0)
-            quant_c(1, 768, 1024)
-            exp_c(2)
-            turn_e(2)
-            mm2(5, 2)
             anchor_mul(2)
             store(1)
-            mm2(7, 0)
-            mm2(7, 1)
+            quant_c(1, 768, 1024)
+            mm2(6, 0)
+            mm2(6, 1)
             exp_c(4)
             turn_e(4)
+            anchor_mul(1)
+            store(0)
             exp_c(5)
             turn_e(5)
             quant_c(2, 768, 1024)
-            mm2(7, 2)
             anchor_mul(4)
-            exp_c(7)
-            mm2(6, 0)
-            mm2(6, 1)
             mm2(6, 2)
             anchor_mul(5)
             store(2)
-            turn_e(7)
             exp_c(6)
+            mm2(7, 0)
+            mm2(7, 1)
+            mm2(7, 2)
+            exp_c(7)
             turn_e(6)
-            anchor_mul(7)
-            store_x(7)
+            turn_e(7)
             anchor_mul(6)
             store_x(6)
+            anchor_mul(7)
+            store_x(7)

@@ -27,8 +27,7 @@ def tile_anchored_log_output_reweighting_s9_kernel(tc, prior, chan_words, chan_s
     nc = tc.nc
     with ExitStack() as ctx:
         keep = ctx.enter_context(tc.tile_pool(name="keep", bufs=1))
-        acc_pool = ctx.enter_context(tc.psum_pool(name="acc_pool", bufs=6))
-        tp_pool = ctx.enter_context(tc.psum_pool(name="tp_pool", bufs=2))
+        psum = ctx.enter_context(tc.psum_pool(name="psum", bufs=1))
 
         def sb(shape, dtype, name):
             return keep.tile(shape, dtype, name=name, align_bytes=64)
@@ -40,10 +39,10 @@ def tile_anchored_log_output_reweighting_s9_kernel(tc, prior, chan_words, chan_s
         p_grp = [sb([P, 512, 4], BF16, f"p_grp{k}") for k in range(KX)]
         p_code = [sb([P, 512], U32, f"p_code{k}") for k in range(KX)]
         p_scale = [sb([P, 512], U8, f"p_scale{k}") for k in range(KX)]
-        w_raw = [sb([P, KX, 1024], U8, f"w_raw{g}") for g in range(GY)]
-        w_code = [sb([P, KX, 1024], U8, f"w_code{g}") for g in range(GY)]
+        w_raw = [sb([P, KX, 1024 * n], U8, f"w_raw{n}") for n in (1, 2)]
+        w_code = [sb([P, 4, KX * 256 * n], U8, f"w_code{n}") for n in (1, 2)]
         ws_raw = sb([P, KX, Y], U8, "ws_raw")
-        w_scale = sb([P, KX, Y], U8, "w_scale")
+        w_scale = sb([P, 4, KX * Y // 4], U8, "w_scale")
         vec_rows = sb([P, 512], BF16, "vec_rows")
         vec_perm = sb([P, 512], BF16, "vec_perm")
         beta_cols = sb([P, GY, 4], F32, "beta_cols")
@@ -58,21 +57,32 @@ def tile_anchored_log_output_reweighting_s9_kernel(tc, prior, chan_words, chan_s
         c_scale = [sb([P, X], U8, f"c_scale{g}") for g in range(GY)]
         anc = sb([P, 4, X], BF16, "anc")
         e_x = [sb([P, 512], F32, f"e_x{i}") for i in range(XT)]
-        o_sb = [sb([P, 4, 256], F32, f"o_sb{i}") for i in range(XT // 2 - 1)]
-        o_last = [sb([P, 4, P], F32, f"o_last{i}") for i in range(2)]
+        o_sb = [sb([P, 4, 256], F32, f"o_sb{i}") for i in range(XT // 2)]
+        o_last = [sb([P, n, P], F32, f"o_last{i}") for i, n in enumerate((4, 2, 2))]
 
         prior_v = prior.rearrange("(j p) x -> p j x", p=P)
         anchor_v = anchor.rearrange("(j p) x -> p j x", p=P)
         out_v = out.rearrange("(j p) x -> p j x", p=P)
-        acc = {}
-        tps = {}
+        free_banks = list(range(8))
+        bank_of = {}
+        held = {}
+
+        def new_bank(key, shape, dtype=F32):
+            bank = free_banks[0]
+            free_banks.remove(bank)
+            bank_of[key] = bank
+            held[key] = psum.tile(shape, dtype, name=f"bank{bank}")
+            return held[key]
+
+        def give_back(key):
+            free_banks.extend([bank_of[key]])
 
         def load_prior(k, j0, j1):
             nc.sync.dma_start(out=p_raw[k][:, j0:j1, :], in_=prior_v[:, j0:j1, 512 * k : 512 * k + 512])
 
-        def load_w(g):
-            src = chan_words[:, :, 1024 * g : 1024 * g + 1024].bitcast(I32)
-            nc.sync.dma_start(out=w_raw[g][:].bitcast(I32), in_=src.rearrange("k p n -> p k n"))
+        def load_w(i):
+            src = chan_words[:, :, 1024 * i : 1024 * (2 * i + 1)].bitcast(I32)
+            nc.sync.dma_start(out=w_raw[i][:].bitcast(I32), in_=src.rearrange("k p n -> p k n"))
 
         def load_c(g, x0, x1):
             rows = channel_t[512 * g : 512 * g + 512, x0:x1].rearrange("(a t e) x -> e a t x", t=4, e=4)
@@ -80,8 +90,7 @@ def tile_anchored_log_output_reweighting_s9_kernel(tc, prior, chan_words, chan_s
                 nc.sync.dma_start(out=c_raw[g][e:P:4, :, x0:x1], in_=rows[e])
 
         def turn_prior(k, h):
-            tp = acc_pool.tile([P, 2, 2, P], F32, name="acc")
-            tps["p", k, h] = tp
+            tp = new_bank(("p", k, h), [P, 2, 2, P])
             words = p_raw[k][:].bitcast(F32)
             for j in range(2):
                 for u in range(2):
@@ -89,33 +98,36 @@ def tile_anchored_log_output_reweighting_s9_kernel(tc, prior, chan_words, chan_s
 
         def copy_prior(k, h, copy):
             dst = p_grp[k][:, 256 * h : 256 * h + 256, :].bitcast(F32).rearrange("p (j b) u -> p j b u", j=2)
-            copy(out=dst, in_=tps["p", k, h][:].rearrange("p j u b -> p j b u"))
+            copy(out=dst, in_=held["p", k, h][:].rearrange("p j u b -> p j b u"))
+            give_back(("p", k, h))
 
-        def quant_prior(k, h):
-            b = slice(256 * h, 256 * h + 256)
+        def quant_prior(k, b0, b1):
+            b = slice(b0, b1)
             nc.vector.quantize_mx(out=p_code[k][:, b].bitcast(E4M3), scales=p_scale[k][:, b], in_=p_grp[k][:, b, :].rearrange("p b t -> p (b t)"))
 
-        def permute_w1(g, k):
+        def permute_w(i):
             nc.vector.tensor_copy(
-                out=w_code[g][:, k, :].bitcast(I32).rearrange("p (t a w) -> p t a w", t=4, w=2),
-                in_=w_raw[g][:, k, :].bitcast(I32).rearrange("p (a t w) -> p t a w", t=4, w=2),
+                out=w_code[i][:].bitcast(I32).rearrange("p t (s w) -> p t s w", w=2),
+                in_=w_raw[i][:].rearrange("p k n -> p (k n)").bitcast(I32).rearrange("p (s t w) -> p t s w", t=4, w=2),
             )
 
         def permute_ws():
             nc.vector.tensor_copy(
-                out=w_scale[:].bitcast(I32).rearrange("p k (t a) -> p k t a", t=4),
-                in_=ws_raw[:].bitcast(I32).rearrange("p k (a t) -> p k t a", t=4),
+                out=w_scale[:].bitcast(I32),
+                in_=ws_raw[:].rearrange("p k y -> p (k y)").bitcast(I32).rearrange("p (s t) -> p t s", t=4),
             )
 
         def mm1(n, k):
             g, t = divmod(n, 4)
             if k == 0:
-                acc["o", n] = acc_pool.tile([P, 512], F32, name="acc")
-            col = (t * GY + g) * P
+                new_bank(("o", n), [P, 512])
+            i = 0 if g == 0 else 1
+            word0 = 256 * ((i + 1) * k + g - i)
+            col = P * (GY * k + g)
             nc.tensor.matmul_mx(
-                out=acc["o", n][:],
-                lhsT=w_code[g][:, k, 256 * t : 256 * t + 256].bitcast(E2M1),
-                lhsT_scale=w_scale[:, k, col : col + P],
+                out=held["o", n][:],
+                lhsT=w_code[i][:, t, word0 : word0 + 256].bitcast(E2M1),
+                lhsT_scale=w_scale[:, t, col : col + P],
                 rhs=p_code[k][:].bitcast(E4M3),
                 rhs_scale=p_scale[k][:],
                 start=(k == 0),
@@ -124,7 +136,8 @@ def tile_anchored_log_output_reweighting_s9_kernel(tc, prior, chan_words, chan_s
 
         def log_o(n):
             g, t = divmod(n, 4)
-            nc.scalar.activation(out=ln_o[g][:, t, :], in_=acc["o", n][:], func=ACT.Ln)
+            nc.scalar.activation(out=ln_o[g][:, t, :], in_=held["o", n][:], func=ACT.Ln)
+            give_back(("o", n))
 
         def beta_mul(g):
             b_row = beta_cols[:, g, :].unsqueeze(1).unsqueeze(3).to_broadcast([P, 128, 4, 4])
@@ -138,11 +151,10 @@ def tile_anchored_log_output_reweighting_s9_kernel(tc, prior, chan_words, chan_s
         def quant_l(g):
             nc.vector.quantize_mx(out=l_code[g][:].bitcast(E5M2), scales=l_scale[g][:], in_=l_grp[g][:].rearrange("p b t -> p (b t)"))
 
-        def group_c(g, q, copy):
-            x0 = 256 * q
+        def group_c(g, x0, x1, copy):
             copy(
-                out=c_grp[g][:, x0 : x0 + 256, :].rearrange("p (c i) t -> p c t i", i=4),
-                in_=c_raw[g][:, :, x0 : x0 + 256].rearrange("p t (c i) -> p c t i", i=4),
+                out=c_grp[g][:, x0:x1, :].rearrange("p (c i) t -> p c t i", i=4),
+                in_=c_raw[g][:, :, x0:x1].rearrange("p t (c i) -> p c t i", i=4),
             )
 
         def quant_c(g, x0, x1):
@@ -154,10 +166,10 @@ def tile_anchored_log_output_reweighting_s9_kernel(tc, prior, chan_words, chan_s
 
         def mm2(x, g):
             if g == 0:
-                acc["c", x] = acc_pool.tile([P, 512], F32, name="acc")
+                new_bank(("c", x), [P, 512])
             col = slice(P * x, P * x + P)
             nc.tensor.matmul_mx(
-                out=acc["c", x][:],
+                out=held["c", x][:],
                 lhsT=c_code[g][:, col].bitcast(E4M3),
                 lhsT_scale=c_scale[g][:, col],
                 rhs=l_code[g][:].bitcast(E5M2),
@@ -167,31 +179,57 @@ def tile_anchored_log_output_reweighting_s9_kernel(tc, prior, chan_words, chan_s
             )
 
         def exp_c(x):
-            nc.scalar.activation(out=e_x[x][:], in_=acc["c", x][:], func=ACT.Exp, scale=-1.0, bias=score_cols[:, x : x + 1])
+            nc.scalar.activation(out=e_x[x][:], in_=held["c", x][:], func=ACT.Exp, scale=-1.0, bias=score_cols[:, x : x + 1])
+            give_back(("c", x))
 
         def turn_e(x):
-            tp = tp_pool.tile([P, 4, P], F32, name="tp")
-            tps["e", x] = tp
+            tp = new_bank(("e", x), [P, 4, P])
             for j in range(4):
                 nc.tensor.transpose(tp[:, j, :], e_x[x][:, P * j : P * j + P], ident[:])
 
         def anchor_mul(x):
             half = P * (x % 2)
             nc.vector.tensor_tensor(
-                out=o_sb[x // 2][:, :, half : half + P] if x < 6 else o_last[x - 6][:], in0=tps["e", x][:], in1=anc[:, :, P * x : P * x + P], op=MULT
+                out=o_sb[x // 2][:, :, half : half + P], in0=held["e", x][:], in1=anc[:, :, P * x : P * x + P], op=MULT
             )
+            give_back(("e", x))
+
+        def anchor_mul_store(x, j0, j1, dst):
+            cols = slice(P * x, P * x + P)
+            nc.vector.tensor_tensor(out=dst[:], in0=held["e", x][:, j0:j1, :], in1=anc[:, j0:j1, cols], op=MULT)
+            if j1 == 4:
+                give_back(("e", x))
+            nc.sync.dma_start(out=out_v[:, j0:j1, cols], in_=dst[:])
 
         def store(i):
             nc.sync.dma_start(out=out_v[:, :, 256 * i : 256 * i + 256], in_=o_sb[i][:])
-
-        def store_x(x):
-            nc.sync.dma_start(out=out_v[:, :, P * x : P * x + P], in_=o_last[x - 6][:])
 
         def scales_in(r):
             nc.sync.dma_start(
                 out=ws_raw[r:P:32, :, :].bitcast(I32),
                 in_=chan_scales[:, r:16:4, :].bitcast(I32).rearrange("k q y -> q k y"),
             )
+
+        def load_anchor(h):
+            nc.sync.dma_start(out=anc[:, :, 512 * h : 512 * h + 512], in_=anchor_v[:, :, 512 * h : 512 * h + 512])
+
+        def permute_vectors():
+            nc.vector.tensor_copy(
+                out=vec_perm[:].rearrange("p (t a e) -> p t a e", t=4, e=4),
+                in_=vec_rows[:].rearrange("p (a t e) -> p t a e", t=4, e=4),
+            )
+
+        def turn_vectors():
+            vec_t = new_bank("vec", [P, 5, P], BF16)
+            for t in range(4):
+                nc.tensor.transpose(vec_t[:, t, :], vec_perm[:, P * t : P * t + P], ident_bf[:])
+            nc.tensor.transpose(vec_t[:, 4, :], vec_rows[:, 0:P], ident_bf[:])
+
+        def copy_vectors():
+            vec_t = held["vec"]
+            nc.vector.tensor_copy(out=beta_cols[:], in_=vec_t[:, 0:4, 0:GY].rearrange("p t g -> p g t"))
+            nc.vector.tensor_copy(out=score_cols[:], in_=vec_t[:, 4, 4 : 4 + XT])
+            give_back("vec")
 
         vcopy, scopy = nc.vector.tensor_copy, nc.scalar.copy
 
@@ -205,165 +243,146 @@ def tile_anchored_log_output_reweighting_s9_kernel(tc, prior, chan_words, chan_s
                 scales_in(r)
             load_prior(1, 0, 2)
             load_prior(1, 2, 4)
-            nc.scalar.activation(out=warm[:, 1:2], in_=warm[:, 0:1], func=ACT.Ln)
+            load_w(1)
+            load_c(0, 0, 1024)
+            load_w(0)
+            load_c(1, 0, 1024)
+            load_c(2, 0, 1024)
+            load_anchor(1)
+            load_anchor(0)
             nc.gpsimd.dma_start(out=vec_rows[0:GY, :], in_=beta.rearrange("(g n) -> g n", g=GY))
             nc.gpsimd.dma_start(out=vec_rows[4 : 4 + XT, 0:P], in_=score.rearrange("(r m) -> r m", m=P))
             make_identity(nc, ident_bf[:])
-            load_w(0)
-            load_c(0, 0, 512)
-            load_c(0, 512, 1024)
-            load_w(1)
-            load_c(1, 0, 1024)
-            load_w(2)
-            load_c(2, 0, 1024)
-            for h in range(2):
-                nc.sync.dma_start(out=anc[:, :, 512 * h : 512 * h + 512], in_=anchor_v[:, :, 512 * h : 512 * h + 512])
             turn_prior(0, 1)
+            nc.scalar.activation(out=warm[:, 1:2], in_=warm[:, 0:1], func=ACT.Ln)
+            copy_prior(0, 1, scopy)
+            quant_prior(0, 256, 512)
             turn_prior(0, 0)
-            turn_prior(1, 1)
-            copy_prior(0, 1, vcopy)
-            copy_prior(0, 0, vcopy)
-            quant_prior(0, 0)
-            permute_ws()
-            permute_w1(0, 0)
+            copy_prior(0, 0, scopy)
             turn_prior(1, 0)
-            vcopy(
-                out=vec_perm[:].rearrange("p (t a e) -> p t a e", t=4, e=4),
-                in_=vec_rows[:].rearrange("p (a t e) -> p t a e", t=4, e=4),
-            )
-            quant_prior(0, 1)
-            mm1(1, 0)
-            copy_prior(1, 1, scopy)
-            quant_prior(1, 1)
-            permute_w1(0, 1)
-            group_c(0, 1, vcopy)
             copy_prior(1, 0, scopy)
-            quant_prior(1, 0)
-            mm1(2, 0)
-            mm1(3, 0)
-            group_c(0, 0, scopy)
-            mm1(3, 1)
-            mm1(1, 1)
-            mm1(0, 0)
-            mm1(0, 1)
-            quant_c(0, 256, 512)
-            group_c(0, 2, vcopy)
-            permute_w1(1, 0)
-            quant_c(0, 512, 768)
-            mm1(2, 1)
-            vec_t = tp_pool.tile([P, 5, P], BF16, name="tp")
-            for t in range(4):
-                nc.tensor.transpose(vec_t[:, t, :], vec_perm[:, P * t : P * t + P], ident_bf[:])
-            nc.tensor.transpose(vec_t[:, 4, :], vec_rows[:, 0:P], ident_bf[:])
+            permute_ws()
+            turn_prior(1, 1)
+            copy_prior(1, 1, scopy)
+            quant_prior(0, 0, 256)
+            permute_w(1)
+            quant_prior(1, 0, 512)
             mm1(4, 0)
-            group_c(0, 3, vcopy)
-            permute_w1(1, 1)
-            vcopy(out=beta_cols[:], in_=vec_t[:, 0:4, 0:GY].rearrange("p t g -> p g t"))
-            vcopy(out=score_cols[:], in_=vec_t[:, 4, 4 : 4 + XT])
             mm1(4, 1)
-            mm1(7, 0)
-            log_o(1)
-            mm1(7, 1)
-            quant_c(0, 0, 256)
-            mm1(6, 0)
-            log_o(0)
-            group_c(1, 0, vcopy)
-            permute_w1(2, 0)
-            mm1(10, 0)
-            log_o(3)
-            log_o(2)
-            group_c(1, 1, scopy)
             log_o(4)
+            group_c(0, 512, 1024, vcopy)
+            mm1(7, 0)
+            group_c(0, 0, 256, scopy)
+            mm1(7, 1)
+            mm1(6, 0)
+            mm1(6, 1)
+            permute_w(0)
+            quant_c(0, 512, 1024)
             mm1(5, 0)
             mm1(5, 1)
-            group_c(1, 2, vcopy)
-            mm1(11, 0)
+            permute_vectors()
+            mm1(3, 0)
+            group_c(0, 256, 512, vcopy)
+            log_o(7)
+            mm1(3, 1)
+            log_o(6)
+            quant_c(0, 0, 512)
+            mm1(1, 0)
+            log_o(3)
             log_o(5)
-            permute_w1(2, 1)
-            mm1(6, 1)
+            mm1(1, 1)
+            log_o(1)
+            turn_vectors()
+            copy_vectors()
+            mm1(2, 0)
+            mm1(2, 1)
+            log_o(2)
+            mm1(0, 0)
+            mm1(0, 1)
+            log_o(0)
+            mm1(10, 0)
+            group_c(1, 512, 768, scopy)
             mm1(8, 0)
             mm1(8, 1)
-            mm1(11, 1)
+            group_c(1, 768, 1024, scopy)
+            group_c(1, 256, 512, vcopy)
+            beta_mul(1)
             mm1(10, 1)
-            quant_c(1, 0, 256)
-            log_o(7)
             mm1(9, 0)
             mm1(9, 1)
-            log_o(6)
-            quant_c(1, 512, 768)
-            quant_c(1, 256, 512)
-            beta_mul(0)
             log_o(8)
-            group_c(2, 0, scopy)
-            log_o(11)
+            mm1(11, 0)
+            mm1(11, 1)
             log_o(10)
-            beta_mul(1)
+            beta_mul(0)
+            quant_c(1, 256, 512)
             quant_l(0)
-            quant_l(1)
-            mm2(2, 0)
-            mm2(0, 0)
-            mm2(0, 1)
-            mm2(4, 0)
-            log_o(9)
-            mm2(4, 1)
-            beta_mul(2)
-            mm2(5, 0)
+            mm2(7, 0)
             mm2(3, 0)
-            mm2(1, 0)
-            group_c(2, 1, scopy)
-            quant_c(2, 256, 512)
-            mm2(2, 1)
-            mm2(3, 1)
-            nc.scalar.activation(out=warm[:, 1:2], in_=warm[:, 0:1], func=ACT.Exp)
-            mm2(5, 1)
-            group_c(2, 3, scopy)
-            mm2(1, 1)
-            quant_l(2)
-            quant_c(2, 0, 256)
-            mm2(3, 2)
-            mm2(2, 2)
-            exp_c(3)
-            group_c(2, 2, vcopy)
-            mm2(0, 2)
-            group_c(1, 3, vcopy)
-            mm2(1, 2)
-            turn_e(3)
-            quant_c(2, 512, 768)
-            exp_c(0)
-            turn_e(0)
-            exp_c(2)
-            mm2(5, 2)
-            turn_e(2)
-            mm2(4, 2)
-            exp_c(1)
-            turn_e(1)
-            anchor_mul(3)
-            quant_c(0, 768, 1024)
-            anchor_mul(0)
-            anchor_mul(2)
-            store(1)
-            quant_c(1, 768, 1024)
+            log_o(9)
+            mm2(5, 0)
+            quant_c(1, 512, 1024)
             mm2(6, 0)
+            quant_l(1)
+            log_o(11)
+            beta_mul(2)
+            group_c(2, 768, 1024, scopy)
+            mm2(1, 0)
+            group_c(1, 0, 256, scopy)
+            mm2(7, 1)
+            quant_c(2, 768, 1024)
+            mm2(0, 0)
+            mm2(3, 1)
             mm2(6, 1)
-            exp_c(4)
-            turn_e(4)
-            anchor_mul(1)
-            store(0)
+            quant_l(2)
+            mm2(2, 0)
+            mm2(4, 0)
+            mm2(2, 1)
+            mm2(5, 1)
+            group_c(2, 256, 512, scopy)
+            quant_c(2, 256, 512)
+            mm2(4, 1)
+            quant_c(1, 0, 256)
+            mm2(7, 2)
+            mm2(6, 2)
+            mm2(3, 2)
+            mm2(0, 1)
+            nc.scalar.activation(out=warm[:, 1:2], in_=warm[:, 0:1], func=ACT.Exp)
+            group_c(2, 512, 768, vcopy)
+            mm2(1, 1)
+            exp_c(7)
+            mm2(2, 2)
+            exp_c(6)
+            turn_e(7)
+            exp_c(2)
+            turn_e(6)
+            group_c(2, 0, 256, vcopy)
+            quant_c(2, 512, 768)
+            mm2(5, 2)
+            anchor_mul(7)
+            anchor_mul(6)
+            store(3)
+            quant_c(2, 0, 256)
+            mm2(4, 2)
+            turn_e(2)
+            exp_c(3)
+            turn_e(3)
+            anchor_mul(2)
+            anchor_mul(3)
+            store(1)
             exp_c(5)
             turn_e(5)
-            quant_c(2, 768, 1024)
-            anchor_mul(4)
-            mm2(6, 2)
+            mm2(0, 2)
             anchor_mul(5)
+            exp_c(4)
+            turn_e(4)
+            exp_c(0)
+            mm2(1, 2)
+            anchor_mul(4)
             store(2)
-            exp_c(6)
-            mm2(7, 0)
-            mm2(7, 1)
-            mm2(7, 2)
-            exp_c(7)
-            turn_e(6)
-            turn_e(7)
-            anchor_mul(6)
-            store_x(6)
-            anchor_mul(7)
-            store_x(7)
+            turn_e(0)
+            anchor_mul_store(0, 0, 4, o_last[0])
+            exp_c(1)
+            turn_e(1)
+            anchor_mul_store(1, 0, 2, o_last[1])
+            anchor_mul_store(1, 2, 4, o_last[2])

@@ -16,6 +16,7 @@ E5M2 = mybir.dt.float8_e5m2_x4
 E2M1 = mybir.dt.float4_e2m1fn_x4
 ACT = mybir.ActivationFunctionType
 MULT = mybir.AluOpType.mult
+ADD = mybir.AluOpType.add
 
 P = 128
 KX = X // 512
@@ -45,7 +46,7 @@ def tile_anchored_log_output_reweighting_s9_kernel(tc, prior, chan_words, chan_s
         w_scale = sb([P, 4, KX * Y // 4], U8, "w_scale")
         vec_rows = sb([P, 512], BF16, "vec_rows")
         vec_perm = sb([P, 512], BF16, "vec_perm")
-        beta_cols = sb([P, GY, 4], F32, "beta_cols")
+        gate = sb([P, GY], F32, "gate")
         score_cols = sb([P, XT], F32, "score_cols")
         ln_o = [sb([P, 4, 512], F32, f"ln_o{g}") for g in range(GY)]
         l_grp = [sb([P, 512, 4], BF16, f"l_grp{g}") for g in range(GY)]
@@ -140,13 +141,15 @@ def tile_anchored_log_output_reweighting_s9_kernel(tc, prior, chan_words, chan_s
             give_back(("o", n))
 
         def beta_mul(g):
-            b_row = beta_cols[:, g, :].unsqueeze(1).unsqueeze(3).to_broadcast([P, 128, 4, 4])
+            b_row = held["vec"][:, 0:4, g].unsqueeze(1).unsqueeze(3).to_broadcast([P, 128, 4, 4])
             nc.vector.tensor_tensor(
                 out=l_grp[g][:].rearrange("p (c i) t -> p c t i", i=4),
                 in0=ln_o[g][:].rearrange("p t (c i) -> p c t i", i=4),
                 in1=b_row,
                 op=MULT,
             )
+            if g == GY - 1:
+                give_back("vec")
 
         def quant_l(g):
             nc.vector.quantize_mx(out=l_code[g][:].bitcast(E5M2), scales=l_scale[g][:], in_=l_grp[g][:].rearrange("p b t -> p (b t)"))
@@ -155,6 +158,17 @@ def tile_anchored_log_output_reweighting_s9_kernel(tc, prior, chan_words, chan_s
             copy(
                 out=c_grp[g][:, x0:x1, :].rearrange("p (c i) t -> p c t i", i=4),
                 in_=c_raw[g][:, :, x0:x1].rearrange("p t (c i) -> p c t i", i=4),
+            )
+
+        def group_c_beside(g, x0, x1, i):
+            nc.vector.memset(gate[:, i : i + 1], 1.0)
+            nc.gpsimd.tensor_scalar(
+                out=c_grp[g][:, x0:x1, :],
+                in0=c_raw[g][:, :, x0:x1].rearrange("p t x -> p x t"),
+                scalar1=gate[:, i : i + 1],
+                scalar2=0.0,
+                op0=MULT,
+                op1=ADD,
             )
 
         def quant_c(g, x0, x1):
@@ -225,11 +239,8 @@ def tile_anchored_log_output_reweighting_s9_kernel(tc, prior, chan_words, chan_s
                 nc.tensor.transpose(vec_t[:, t, :], vec_perm[:, P * t : P * t + P], ident_bf[:])
             nc.tensor.transpose(vec_t[:, 4, :], vec_rows[:, 0:P], ident_bf[:])
 
-        def copy_vectors():
-            vec_t = held["vec"]
-            nc.vector.tensor_copy(out=beta_cols[:], in_=vec_t[:, 0:4, 0:GY].rearrange("p t g -> p g t"))
-            nc.vector.tensor_copy(out=score_cols[:], in_=vec_t[:, 4, 4 : 4 + XT])
-            give_back("vec")
+        def copy_score():
+            nc.vector.tensor_copy(out=score_cols[:], in_=held["vec"][:, 4, 4 : 4 + XT])
 
         vcopy, scopy = nc.vector.tensor_copy, nc.scalar.copy
 
@@ -241,11 +252,11 @@ def tile_anchored_log_output_reweighting_s9_kernel(tc, prior, chan_words, chan_s
             load_prior(0, 0, 4)
             for r in range(4):
                 scales_in(r)
-            load_prior(1, 0, 2)
             load_prior(1, 2, 4)
-            load_w(1)
-            load_c(0, 0, 1024)
+            load_prior(1, 0, 2)
             load_w(0)
+            load_c(0, 0, 1024)
+            load_w(1)
             load_c(1, 0, 1024)
             load_c(2, 0, 1024)
             load_anchor(1)
@@ -255,131 +266,129 @@ def tile_anchored_log_output_reweighting_s9_kernel(tc, prior, chan_words, chan_s
             make_identity(nc, ident_bf[:])
             turn_prior(0, 1)
             nc.scalar.activation(out=warm[:, 1:2], in_=warm[:, 0:1], func=ACT.Ln)
+            permute_ws()
             copy_prior(0, 1, scopy)
-            quant_prior(0, 256, 512)
             turn_prior(0, 0)
             copy_prior(0, 0, scopy)
+            permute_w(0)
+            turn_prior(1, 1)
+            quant_prior(0, 0, 512)
             turn_prior(1, 0)
             copy_prior(1, 0, scopy)
-            permute_ws()
-            turn_prior(1, 1)
-            copy_prior(1, 1, scopy)
-            quant_prior(0, 0, 256)
-            permute_w(1)
+            copy_prior(1, 1, vcopy)
             quant_prior(1, 0, 512)
-            mm1(4, 0)
-            mm1(4, 1)
-            log_o(4)
-            group_c(0, 512, 1024, vcopy)
-            mm1(7, 0)
-            group_c(0, 0, 256, scopy)
-            mm1(7, 1)
-            mm1(6, 0)
-            mm1(6, 1)
-            permute_w(0)
-            quant_c(0, 512, 1024)
-            mm1(5, 0)
-            mm1(5, 1)
-            permute_vectors()
-            mm1(3, 0)
-            group_c(0, 256, 512, vcopy)
-            log_o(7)
-            mm1(3, 1)
-            log_o(6)
-            quant_c(0, 0, 512)
-            mm1(1, 0)
-            log_o(3)
-            log_o(5)
-            mm1(1, 1)
-            log_o(1)
-            turn_vectors()
-            copy_vectors()
             mm1(2, 0)
+            group_c(0, 0, 512, vcopy)
+            group_c(0, 512, 768, vcopy)
+            permute_w(1)
+            permute_vectors()
+            quant_c(0, 0, 512)
+            mm1(3, 0)
+            mm1(1, 0)
             mm1(2, 1)
-            log_o(2)
+            mm1(1, 1)
+            group_c(0, 768, 1024, scopy)
+            mm1(3, 1)
             mm1(0, 0)
             mm1(0, 1)
+            mm1(5, 0)
+            mm1(5, 1)
+            turn_vectors()
+            quant_c(0, 512, 1024)
+            log_o(2)
+            mm1(6, 0)
+            log_o(1)
+            log_o(3)
+            group_c_beside(1, 768, 1024, 0)
+            mm1(6, 1)
             log_o(0)
-            mm1(10, 0)
-            group_c(1, 512, 768, scopy)
-            mm1(8, 0)
-            mm1(8, 1)
-            group_c(1, 768, 1024, scopy)
-            group_c(1, 256, 512, vcopy)
-            beta_mul(1)
-            mm1(10, 1)
-            mm1(9, 0)
-            mm1(9, 1)
-            log_o(8)
-            mm1(11, 0)
-            mm1(11, 1)
-            log_o(10)
+            mm1(4, 0)
             beta_mul(0)
+            mm1(11, 0)
+            mm1(4, 1)
+            mm1(11, 1)
+            log_o(5)
+            group_c(1, 256, 512, scopy)
             quant_c(1, 256, 512)
+            mm1(7, 0)
+            log_o(6)
             quant_l(0)
-            mm2(7, 0)
-            mm2(3, 0)
+            log_o(4)
+            mm1(9, 0)
+            mm1(7, 1)
+            log_o(7)
+            group_c_beside(2, 0, 256, 1)
+            mm1(9, 1)
             log_o(9)
-            mm2(5, 0)
-            quant_c(1, 512, 1024)
-            mm2(6, 0)
-            quant_l(1)
+            beta_mul(1)
+            mm1(10, 0)
+            mm1(8, 0)
             log_o(11)
-            beta_mul(2)
-            group_c(2, 768, 1024, scopy)
-            mm2(1, 0)
-            group_c(1, 0, 256, scopy)
-            mm2(7, 1)
-            quant_c(2, 768, 1024)
-            mm2(0, 0)
-            mm2(3, 1)
-            mm2(6, 1)
-            quant_l(2)
+            mm1(8, 1)
             mm2(2, 0)
+            group_c(1, 512, 768, scopy)
+            mm1(10, 1)
+            quant_c(1, 512, 1024)
+            log_o(10)
+            log_o(8)
+            group_c(2, 512, 768, scopy)
+            mm2(5, 0)
+            quant_l(1)
+            group_c_beside(2, 256, 512, 2)
+            group_c(2, 768, 1024, scopy)
+            beta_mul(2)
+            quant_c(2, 256, 512)
+            quant_l(2)
+            mm2(1, 0)
+            mm2(6, 0)
+            mm2(6, 1)
+            copy_score()
+            quant_c(2, 512, 1024)
+            mm2(7, 0)
+            mm2(7, 1)
             mm2(4, 0)
             mm2(2, 1)
-            mm2(5, 1)
-            group_c(2, 256, 512, scopy)
-            quant_c(2, 256, 512)
-            mm2(4, 1)
-            quant_c(1, 0, 256)
-            mm2(7, 2)
-            mm2(6, 2)
-            mm2(3, 2)
-            mm2(0, 1)
+            mm2(3, 0)
             nc.scalar.activation(out=warm[:, 1:2], in_=warm[:, 0:1], func=ACT.Exp)
-            group_c(2, 512, 768, vcopy)
-            mm2(1, 1)
-            exp_c(7)
-            mm2(2, 2)
-            exp_c(6)
-            turn_e(7)
-            exp_c(2)
-            turn_e(6)
-            group_c(2, 0, 256, vcopy)
-            quant_c(2, 512, 768)
-            mm2(5, 2)
-            anchor_mul(7)
-            anchor_mul(6)
-            store(3)
+            group_c(1, 0, 256, vcopy)
+            mm2(4, 1)
+            mm2(0, 0)
+            mm2(3, 1)
+            mm2(5, 1)
+            mm2(3, 2)
             quant_c(2, 0, 256)
-            mm2(4, 2)
-            turn_e(2)
             exp_c(3)
+            mm2(2, 2)
+            mm2(4, 2)
+            mm2(5, 2)
+            quant_c(1, 0, 256)
+            exp_c(2)
+            mm2(6, 2)
             turn_e(3)
-            anchor_mul(2)
-            anchor_mul(3)
-            store(1)
+            turn_e(2)
+            mm2(7, 2)
             exp_c(5)
             turn_e(5)
-            mm2(0, 2)
-            anchor_mul(5)
             exp_c(4)
             turn_e(4)
-            exp_c(0)
-            mm2(1, 2)
+            anchor_mul(3)
+            mm2(0, 1)
+            mm2(0, 2)
+            anchor_mul(2)
+            store(1)
+            anchor_mul(5)
             anchor_mul(4)
             store(2)
+            exp_c(7)
+            exp_c(6)
+            turn_e(7)
+            turn_e(6)
+            mm2(1, 1)
+            mm2(1, 2)
+            anchor_mul(7)
+            exp_c(0)
+            anchor_mul(6)
+            store(3)
             turn_e(0)
             anchor_mul_store(0, 0, 4, o_last[0])
             exp_c(1)

@@ -52,14 +52,15 @@ def tile_anchored_log_output_reweighting_s9_kernel(tc, prior, chan_words, chan_s
         l_grp = [sb([P, 512, 4], BF16, f"l_grp{g}") for g in range(GY)]
         l_code = [sb([P, 512], U32, f"l_code{g}") for g in range(GY)]
         l_scale = [sb([P, 512], U8, f"l_scale{g}") for g in range(GY)]
-        c_raw = [sb([P, 4, X], BF16, f"c_raw{g}") for g in range(GY)]
+        c_raw0 = [sb([P, 4, 512], BF16, f"c_raw0{h}") for h in range(2)]
+        c_raw = [None] + [sb([P, 4, X], BF16, f"c_raw{g}") for g in range(1, GY)]
         c_grp = [sb([P, X, 4], BF16, f"c_grp{g}") for g in range(GY)]
         c_code = [sb([P, X], U32, f"c_code{g}") for g in range(GY)]
         c_scale = [sb([P, X], U8, f"c_scale{g}") for g in range(GY)]
         anc = sb([P, 4, X], BF16, "anc")
         e_x = [sb([P, 512], F32, f"e_x{i}") for i in range(XT)]
-        o_sb = [sb([P, 4, 256], F32, f"o_sb{i}") for i in range(XT // 2)]
-        o_last = [sb([P, n, P], F32, f"o_last{i}") for i, n in enumerate((4, 2, 2))]
+        o_sb = [sb([P, 4, 256], F32, f"o_sb{i}") for i in range(XT // 2 - 1)]
+        o_half = [[sb([P, 2, P], F32, f"o_half{x}{h}") for h in range(2)] for x in range(2)]
 
         prior_v = prior.rearrange("(j p) x -> p j x", p=P)
         anchor_v = anchor.rearrange("(j p) x -> p j x", p=P)
@@ -85,10 +86,16 @@ def tile_anchored_log_output_reweighting_s9_kernel(tc, prior, chan_words, chan_s
             src = chan_words[:, :, 1024 * i : 1024 * (2 * i + 1)].bitcast(I32)
             nc.sync.dma_start(out=w_raw[i][:].bitcast(I32), in_=src.rearrange("k p n -> p k n"))
 
+        def c_cols(g, x0, x1):
+            if g == 0:
+                return c_raw0[x0 // 512][:, :, x0 % 512 : x0 % 512 + x1 - x0]
+            return c_raw[g][:, :, x0:x1]
+
         def load_c(g, x0, x1):
             rows = channel_t[512 * g : 512 * g + 512, x0:x1].rearrange("(a t e) x -> e a t x", t=4, e=4)
+            dst = c_cols(g, x0, x1)
             for e in range(4):
-                nc.sync.dma_start(out=c_raw[g][e:P:4, :, x0:x1], in_=rows[e])
+                nc.sync.dma_start(out=dst[e:P:4, :, :], in_=rows[e])
 
         def turn_prior(k, h):
             tp = new_bank(("p", k, h), [P, 2, 2, P])
@@ -157,14 +164,14 @@ def tile_anchored_log_output_reweighting_s9_kernel(tc, prior, chan_words, chan_s
         def group_c(g, x0, x1, copy):
             copy(
                 out=c_grp[g][:, x0:x1, :].rearrange("p (c i) t -> p c t i", i=4),
-                in_=c_raw[g][:, :, x0:x1].rearrange("p t (c i) -> p c t i", i=4),
+                in_=c_cols(g, x0, x1).rearrange("p t (c i) -> p c t i", i=4),
             )
 
         def group_c_beside(g, x0, x1, i):
             nc.vector.memset(gate[:, i : i + 1], 1.0)
             nc.gpsimd.tensor_scalar(
                 out=c_grp[g][:, x0:x1, :],
-                in0=c_raw[g][:, :, x0:x1].rearrange("p t x -> p x t"),
+                in0=c_cols(g, x0, x1).rearrange("p t x -> p x t"),
                 scalar1=gate[:, i : i + 1],
                 scalar2=0.0,
                 op0=MULT,
@@ -192,31 +199,35 @@ def tile_anchored_log_output_reweighting_s9_kernel(tc, prior, chan_words, chan_s
                 stop=(g == GY - 1),
             )
 
-        def exp_c(x):
-            nc.scalar.activation(out=e_x[x][:], in_=held["c", x][:], func=ACT.Exp, scale=-1.0, bias=score_cols[:, x : x + 1])
-            give_back(("c", x))
+        def exp_c(x, j0=0, j1=4):
+            b = slice(P * j0, P * j1)
+            nc.scalar.activation(
+                out=e_x[x][:, b], in_=held["c", x][:, b], func=ACT.Exp, scale=-1.0, bias=score_cols[:, x : x + 1]
+            )
+            if j1 == 4:
+                give_back(("c", x))
 
-        def turn_e(x):
-            tp = new_bank(("e", x), [P, 4, P])
-            for j in range(4):
-                nc.tensor.transpose(tp[:, j, :], e_x[x][:, P * j : P * j + P], ident[:])
+        def turn_e(x, j0=0, j1=4):
+            tp = new_bank(("e", x, j0), [P, j1 - j0, P])
+            for j in range(j0, j1):
+                nc.tensor.transpose(tp[:, j - j0, :], e_x[x][:, P * j : P * j + P], ident[:])
 
         def anchor_mul(x):
             half = P * (x % 2)
             nc.vector.tensor_tensor(
-                out=o_sb[x // 2][:, :, half : half + P], in0=held["e", x][:], in1=anc[:, :, P * x : P * x + P], op=MULT
+                out=o_sb[x // 2][:, :, half : half + P], in0=held["e", x, 0][:], in1=anc[:, :, P * x : P * x + P], op=MULT
             )
-            give_back(("e", x))
-
-        def anchor_mul_store(x, j0, j1, dst):
-            cols = slice(P * x, P * x + P)
-            nc.vector.tensor_tensor(out=dst[:], in0=held["e", x][:, j0:j1, :], in1=anc[:, j0:j1, cols], op=MULT)
-            if j1 == 4:
-                give_back(("e", x))
-            nc.sync.dma_start(out=out_v[:, j0:j1, cols], in_=dst[:])
+            give_back(("e", x, 0))
 
         def store(i):
             nc.sync.dma_start(out=out_v[:, :, 256 * i : 256 * i + 256], in_=o_sb[i][:])
+
+        def anchor_mul_store(x, j0, j1):
+            cols = slice(P * x, P * x + P)
+            half = o_half[x - 6][j0 // 2]
+            nc.vector.tensor_tensor(out=half[:], in0=held["e", x, j0][:], in1=anc[:, j0:j1, cols], op=MULT)
+            give_back(("e", x, j0))
+            nc.sync.dma_start(out=out_v[:, j0:j1, cols], in_=half[:])
 
         def scales_in(r):
             nc.sync.dma_start(
@@ -227,8 +238,8 @@ def tile_anchored_log_output_reweighting_s9_kernel(tc, prior, chan_words, chan_s
         def load_anchor(h):
             nc.sync.dma_start(out=anc[:, :, 512 * h : 512 * h + 512], in_=anchor_v[:, :, 512 * h : 512 * h + 512])
 
-        def permute_vectors():
-            nc.vector.tensor_copy(
+        def permute_vectors(copy):
+            copy(
                 out=vec_perm[:].rearrange("p (t a e) -> p t a e", t=4, e=4),
                 in_=vec_rows[:].rearrange("p (a t e) -> p t a e", t=4, e=4),
             )
@@ -239,8 +250,8 @@ def tile_anchored_log_output_reweighting_s9_kernel(tc, prior, chan_words, chan_s
                 nc.tensor.transpose(vec_t[:, t, :], vec_perm[:, P * t : P * t + P], ident_bf[:])
             nc.tensor.transpose(vec_t[:, 4, :], vec_rows[:, 0:P], ident_bf[:])
 
-        def copy_score():
-            nc.vector.tensor_copy(out=score_cols[:], in_=held["vec"][:, 4, 4 : 4 + XT])
+        def copy_score(copy):
+            copy(out=score_cols[:], in_=held["vec"][:, 4, 4 : 4 + XT])
 
         vcopy, scopy = nc.vector.tensor_copy, nc.scalar.copy
 
@@ -249,149 +260,160 @@ def tile_anchored_log_output_reweighting_s9_kernel(tc, prior, chan_words, chan_s
             nc.vector.memset(warm[:], 1.0)
             nc.vector.memset(vec_rows[:], 0.0)
             make_identity(nc, ident[:])
-            load_prior(0, 0, 4)
+            load_prior(0, 2, 4)
+            load_prior(0, 0, 2)
             for r in range(4):
                 scales_in(r)
-            load_prior(1, 2, 4)
             load_prior(1, 0, 2)
+            load_prior(1, 2, 4)
             load_w(0)
-            load_c(0, 0, 1024)
+            load_c(0, 0, 512)
             load_w(1)
+            load_c(0, 512, 1024)
             load_c(1, 0, 1024)
             load_c(2, 0, 1024)
-            load_anchor(1)
             load_anchor(0)
+            load_anchor(1)
             nc.gpsimd.dma_start(out=vec_rows[0:GY, :], in_=beta.rearrange("(g n) -> g n", g=GY))
             nc.gpsimd.dma_start(out=vec_rows[4 : 4 + XT, 0:P], in_=score.rearrange("(r m) -> r m", m=P))
             make_identity(nc, ident_bf[:])
-            turn_prior(0, 1)
             nc.scalar.activation(out=warm[:, 1:2], in_=warm[:, 0:1], func=ACT.Ln)
-            permute_ws()
-            copy_prior(0, 1, scopy)
+            turn_prior(0, 1)
+            group_c_beside(1, 512, 768, 0)
             turn_prior(0, 0)
-            copy_prior(0, 0, scopy)
-            permute_w(0)
-            turn_prior(1, 1)
-            quant_prior(0, 0, 512)
+            copy_prior(0, 1, vcopy)
+            quant_prior(0, 256, 512)
             turn_prior(1, 0)
-            copy_prior(1, 0, scopy)
-            copy_prior(1, 1, vcopy)
-            quant_prior(1, 0, 512)
-            mm1(2, 0)
-            group_c(0, 0, 512, vcopy)
-            group_c(0, 512, 768, vcopy)
-            permute_w(1)
-            permute_vectors()
-            quant_c(0, 0, 512)
-            mm1(3, 0)
-            mm1(1, 0)
-            mm1(2, 1)
-            mm1(1, 1)
-            group_c(0, 768, 1024, scopy)
-            mm1(3, 1)
+            turn_prior(1, 1)
+            permute_ws()
+            copy_prior(0, 0, scopy)
+            quant_prior(0, 0, 256)
+            copy_prior(1, 1, scopy)
+            permute_w(0)
+            quant_prior(1, 256, 512)
             mm1(0, 0)
+            mm1(1, 0)
+            group_c_beside(1, 256, 512, 1)
+            copy_prior(1, 0, scopy)
+            quant_prior(1, 0, 256)
+            group_c(0, 256, 512, scopy)
             mm1(0, 1)
-            mm1(5, 0)
-            mm1(5, 1)
-            turn_vectors()
-            quant_c(0, 512, 1024)
-            log_o(2)
-            mm1(6, 0)
-            log_o(1)
-            log_o(3)
-            group_c_beside(1, 768, 1024, 0)
-            mm1(6, 1)
+            mm1(1, 1)
+            group_c(0, 0, 256, vcopy)
+            permute_w(1)
+            quant_c(0, 0, 512)
             log_o(0)
+            log_o(1)
+            mm1(3, 0)
+            mm1(3, 1)
+            group_c(0, 512, 768, vcopy)
+            log_o(3)
+            mm1(2, 0)
+            mm1(2, 1)
             mm1(4, 0)
-            beta_mul(0)
-            mm1(11, 0)
-            mm1(4, 1)
-            mm1(11, 1)
-            log_o(5)
-            group_c(1, 256, 512, scopy)
-            quant_c(1, 256, 512)
             mm1(7, 0)
-            log_o(6)
-            quant_l(0)
-            log_o(4)
-            mm1(9, 0)
             mm1(7, 1)
+            permute_vectors(scopy)
+            turn_vectors()
+            log_o(2)
+            mm1(4, 1)
+            mm1(6, 0)
+            mm1(6, 1)
+            mm1(5, 0)
+            group_c(0, 768, 1024, vcopy)
+            quant_c(0, 512, 768)
             log_o(7)
-            group_c_beside(2, 0, 256, 1)
-            mm1(9, 1)
-            log_o(9)
-            beta_mul(1)
+            log_o(4)
+            mm1(5, 1)
+            mm1(11, 0)
             mm1(10, 0)
-            mm1(8, 0)
-            log_o(11)
-            mm1(8, 1)
-            mm2(2, 0)
-            group_c(1, 512, 768, scopy)
             mm1(10, 1)
-            quant_c(1, 512, 1024)
-            log_o(10)
-            log_o(8)
-            group_c(2, 512, 768, scopy)
-            mm2(5, 0)
-            quant_l(1)
-            group_c_beside(2, 256, 512, 2)
-            group_c(2, 768, 1024, scopy)
-            beta_mul(2)
-            quant_c(2, 256, 512)
-            quant_l(2)
-            mm2(1, 0)
-            mm2(6, 0)
-            mm2(6, 1)
-            copy_score()
-            quant_c(2, 512, 1024)
-            mm2(7, 0)
-            mm2(7, 1)
-            mm2(4, 0)
-            mm2(2, 1)
+            mm1(11, 1)
+            log_o(6)
+            quant_c(0, 768, 1024)
+            beta_mul(0)
+            mm1(8, 0)
+            log_o(5)
+            beta_mul(1)
+            mm1(8, 1)
+            group_c(1, 0, 256, scopy)
+            mm1(9, 0)
+            mm1(9, 1)
+            quant_l(0)
             mm2(3, 0)
-            nc.scalar.activation(out=warm[:, 1:2], in_=warm[:, 0:1], func=ACT.Exp)
-            group_c(1, 0, 256, vcopy)
-            mm2(4, 1)
-            mm2(0, 0)
+            quant_c(1, 0, 512)
+            log_o(8)
+            mm2(5, 0)
+            mm2(1, 0)
+            mm2(2, 0)
+            log_o(9)
+            quant_l(1)
+            log_o(11)
+            group_c_beside(2, 0, 256, 2)
+            log_o(10)
+            mm2(6, 0)
             mm2(3, 1)
+            mm2(2, 1)
+            beta_mul(2)
+            mm2(0, 0)
+            mm2(0, 1)
+            mm2(7, 0)
+            nc.scalar.activation(out=warm[:, 1:2], in_=warm[:, 0:1], func=ACT.Exp)
+            quant_c(1, 512, 768)
+            group_c(2, 256, 512, scopy)
+            quant_l(2)
+            group_c(2, 512, 768, scopy)
+            quant_c(2, 512, 768)
+            mm2(4, 0)
+            copy_score(vcopy)
+            mm2(4, 1)
+            quant_c(2, 0, 512)
             mm2(5, 1)
-            mm2(3, 2)
-            quant_c(2, 0, 256)
-            exp_c(3)
-            mm2(2, 2)
-            mm2(4, 2)
+            group_c(1, 768, 1024, vcopy)
+            mm2(1, 1)
             mm2(5, 2)
-            quant_c(1, 0, 256)
-            exp_c(2)
-            mm2(6, 2)
-            turn_e(3)
-            turn_e(2)
-            mm2(7, 2)
+            mm2(4, 2)
+            mm2(3, 2)
+            group_c(2, 768, 1024, scopy)
+            mm2(2, 2)
+            quant_c(2, 768, 1024)
+            quant_c(1, 768, 1024)
             exp_c(5)
+            mm2(1, 2)
             turn_e(5)
             exp_c(4)
             turn_e(4)
-            anchor_mul(3)
-            mm2(0, 1)
+            exp_c(3)
             mm2(0, 2)
-            anchor_mul(2)
-            store(1)
             anchor_mul(5)
+            exp_c(2)
             anchor_mul(4)
             store(2)
-            exp_c(7)
-            exp_c(6)
-            turn_e(7)
-            turn_e(6)
-            mm2(1, 1)
-            mm2(1, 2)
-            anchor_mul(7)
-            exp_c(0)
-            anchor_mul(6)
-            store(3)
-            turn_e(0)
-            anchor_mul_store(0, 0, 4, o_last[0])
+            turn_e(3)
             exp_c(1)
+            anchor_mul(3)
+            turn_e(2)
+            exp_c(0)
+            mm2(6, 1)
+            anchor_mul(2)
+            store(1)
             turn_e(1)
-            anchor_mul_store(1, 0, 2, o_last[1])
-            anchor_mul_store(1, 2, 4, o_last[2])
+            turn_e(0)
+            mm2(6, 2)
+            mm2(7, 1)
+            exp_c(6, 0, 2)
+            anchor_mul(1)
+            exp_c(6, 2, 4)
+            mm2(7, 2)
+            exp_c(7, 0, 2)
+            anchor_mul(0)
+            store(0)
+            exp_c(7, 2, 4)
+            turn_e(6, 0, 2)
+            anchor_mul_store(6, 0, 2)
+            turn_e(6, 2, 4)
+            anchor_mul_store(6, 2, 4)
+            turn_e(7, 0, 2)
+            anchor_mul_store(7, 0, 2)
+            turn_e(7, 2, 4)
+            anchor_mul_store(7, 2, 4)

from contextlib import ExitStack

import concourse.mybir as mybir
from concourse.masks import make_identity

B, X, Y = 512, 1024, 1536
FLOPS = 2 * B * X * Y * 2

F32 = mybir.dt.float32
BF16 = mybir.dt.bfloat16
I32 = mybir.dt.int32
U32 = mybir.dt.uint32
U8 = mybir.dt.uint8
E4M3 = mybir.dt.float8_e4m3fn_x4
E5M2 = mybir.dt.float8_e5m2_x4
E2M1 = mybir.dt.float4_e2m1fn_x4
ACT = mybir.ActivationFunctionType
MULT = mybir.AluOpType.mult
ADD = mybir.AluOpType.add

P = 128
KX = X // 512
GY = Y // 512
XT = X // P


def tile_anchored_log_output_reweighting_s9_kernel(tc, prior, chan_words, chan_scales, beta, channel_t, score, anchor, out):
    nc = tc.nc
    with ExitStack() as ctx:
        keep = ctx.enter_context(tc.tile_pool(name="keep", bufs=1))
        psum = ctx.enter_context(tc.psum_pool(name="psum", bufs=1))

        def sb(shape, dtype, name):
            return keep.tile(shape, dtype, name=name, align_bytes=64)

        ident = sb([P, P], F32, "ident")
        ident_bf = sb([P, P], BF16, "ident_bf")
        warm = sb([P, 2], F32, "warm")
        p_raw = [sb([P, 4, 512], BF16, f"p_raw{k}") for k in range(KX)]
        p_grp = [sb([P, 512, 4], BF16, f"p_grp{k}") for k in range(KX)]
        p_code = [sb([P, 512], U32, f"p_code{k}") for k in range(KX)]
        p_scale = [sb([P, 512], U8, f"p_scale{k}") for k in range(KX)]
        w_raw = [sb([P, KX, 1024 * n], U8, f"w_raw{n}") for n in (1, 2)]
        w_code = [sb([P, 4, KX * 256 * n], U8, f"w_code{n}") for n in (1, 2)]
        ws_raw = sb([P, KX, Y], U8, "ws_raw")
        w_scale = sb([P, 4, KX * Y // 4], U8, "w_scale")
        vec_rows = sb([P, 512], BF16, "vec_rows")
        vec_perm = sb([P, 512], BF16, "vec_perm")
        gate = sb([P, GY], F32, "gate")
        score_cols = sb([P, XT], F32, "score_cols")
        ln_o = [sb([P, 4, 512], F32, f"ln_o{g}") for g in range(GY)]
        l_grp = [sb([P, 512, 4], BF16, f"l_grp{g}") for g in range(GY)]
        l_code = [sb([P, 512], U32, f"l_code{g}") for g in range(GY)]
        l_scale = [sb([P, 512], U8, f"l_scale{g}") for g in range(GY)]
        c_raw0 = [sb([P, 4, 512], BF16, f"c_raw0{h}") for h in range(2)]
        c_raw = [None] + [sb([P, 4, X], BF16, f"c_raw{g}") for g in range(1, GY)]
        c_grp = [sb([P, X, 4], BF16, f"c_grp{g}") for g in range(GY)]
        c_code = [sb([P, X], U32, f"c_code{g}") for g in range(GY)]
        c_scale = [sb([P, X], U8, f"c_scale{g}") for g in range(GY)]
        anc = sb([P, 4, X], BF16, "anc")
        e_x = [sb([P, 512], F32, f"e_x{i}") for i in range(XT)]
        o_sb = [sb([P, 4, 256], F32, f"o_sb{i}") for i in range(XT // 2 - 1)]
        o_half = [[sb([P, 2, P], F32, f"o_half{x}{h}") for h in range(2)] for x in range(2)]

        prior_v = prior.rearrange("(j p) x -> p j x", p=P)
        anchor_v = anchor.rearrange("(j p) x -> p j x", p=P)
        out_v = out.rearrange("(j p) x -> p j x", p=P)
        free_banks = list(range(8))
        bank_of = {}
        held = {}

        def new_bank(key, shape, dtype=F32):
            bank = free_banks[0]
            free_banks.remove(bank)
            bank_of[key] = bank
            held[key] = psum.tile(shape, dtype, name=f"bank{bank}")
            return held[key]

        def give_back(key):
            free_banks.extend([bank_of[key]])

        def load_prior(k, j0, j1):
            nc.sync.dma_start(out=p_raw[k][:, j0:j1, :], in_=prior_v[:, j0:j1, 512 * k : 512 * k + 512])

        def load_w(i):
            src = chan_words[:, :, 1024 * i : 1024 * (2 * i + 1)].bitcast(I32)
            nc.sync.dma_start(out=w_raw[i][:].bitcast(I32), in_=src.rearrange("k p n -> p k n"))

        def c_cols(g, x0, x1):
            if g == 0:
                return c_raw0[x0 // 512][:, :, x0 % 512 : x0 % 512 + x1 - x0]
            return c_raw[g][:, :, x0:x1]

        def load_c(g, x0, x1):
            rows = channel_t[512 * g : 512 * g + 512, x0:x1].rearrange("(a t e) x -> e a t x", t=4, e=4)
            dst = c_cols(g, x0, x1)
            for e in range(4):
                nc.sync.dma_start(out=dst[e:P:4, :, :], in_=rows[e])

        def turn_prior(k, h):
            tp = new_bank(("p", k, h), [P, 2, 2, P])
            words = p_raw[k][:].bitcast(F32)
            for j in range(2):
                for u in range(2):
                    nc.tensor.transpose(tp[:, j, u, :], words[:, 2 * h + j, u:256:2], ident[:])

        def copy_prior(k, h, copy):
            dst = p_grp[k][:, 256 * h : 256 * h + 256, :].bitcast(F32).rearrange("p (j b) u -> p j b u", j=2)
            copy(out=dst, in_=held["p", k, h][:].rearrange("p j u b -> p j b u"))
            give_back(("p", k, h))

        def quant_prior(k, b0, b1):
            b = slice(b0, b1)
            nc.vector.quantize_mx(out=p_code[k][:, b].bitcast(E4M3), scales=p_scale[k][:, b], in_=p_grp[k][:, b, :].rearrange("p b t -> p (b t)"))

        def permute_w(i):
            nc.vector.tensor_copy(
                out=w_code[i][:].bitcast(I32).rearrange("p t (s w) -> p t s w", w=2),
                in_=w_raw[i][:].rearrange("p k n -> p (k n)").bitcast(I32).rearrange("p (s t w) -> p t s w", t=4, w=2),
            )

        def permute_ws():
            nc.vector.tensor_copy(
                out=w_scale[:].bitcast(I32),
                in_=ws_raw[:].rearrange("p k y -> p (k y)").bitcast(I32).rearrange("p (s t) -> p t s", t=4),
            )

        def mm1(n, k):
            g, t = divmod(n, 4)
            if k == 0:
                new_bank(("o", n), [P, 512])
            i = 0 if g == 0 else 1
            word0 = 256 * ((i + 1) * k + g - i)
            col = P * (GY * k + g)
            nc.tensor.matmul_mx(
                out=held["o", n][:],
                lhsT=w_code[i][:, t, word0 : word0 + 256].bitcast(E2M1),
                lhsT_scale=w_scale[:, t, col : col + P],
                rhs=p_code[k][:].bitcast(E4M3),
                rhs_scale=p_scale[k][:],
                start=(k == 0),
                stop=(k == KX - 1),
            )

        def log_o(n):
            g, t = divmod(n, 4)
            nc.scalar.activation(out=ln_o[g][:, t, :], in_=held["o", n][:], func=ACT.Ln)
            give_back(("o", n))

        def beta_mul(g):
            b_row = held["vec"][:, 0:4, g].unsqueeze(1).unsqueeze(3).to_broadcast([P, 128, 4, 4])
            nc.vector.tensor_tensor(
                out=l_grp[g][:].rearrange("p (c i) t -> p c t i", i=4),
                in0=ln_o[g][:].rearrange("p t (c i) -> p c t i", i=4),
                in1=b_row,
                op=MULT,
            )
            if g == GY - 1:
                give_back("vec")

        def quant_l(g):
            nc.vector.quantize_mx(out=l_code[g][:].bitcast(E5M2), scales=l_scale[g][:], in_=l_grp[g][:].rearrange("p b t -> p (b t)"))

        def group_c(g, x0, x1, copy):
            copy(
                out=c_grp[g][:, x0:x1, :].rearrange("p (c i) t -> p c t i", i=4),
                in_=c_cols(g, x0, x1).rearrange("p t (c i) -> p c t i", i=4),
            )

        def group_c_beside(g, x0, x1, i):
            nc.vector.memset(gate[:, i : i + 1], 1.0)
            nc.gpsimd.tensor_scalar(
                out=c_grp[g][:, x0:x1, :],
                in0=c_cols(g, x0, x1).rearrange("p t x -> p x t"),
                scalar1=gate[:, i : i + 1],
                scalar2=0.0,
                op0=MULT,
                op1=ADD,
            )

        def quant_c(g, x0, x1):
            nc.vector.quantize_mx(
                out=c_code[g][:, x0:x1].bitcast(E4M3),
                scales=c_scale[g][:, x0:x1],
                in_=c_grp[g][:, x0:x1, :].rearrange("p x t -> p (x t)"),
            )

        def mm2(x, g):
            if g == 0:
                new_bank(("c", x), [P, 512])
            col = slice(P * x, P * x + P)
            nc.tensor.matmul_mx(
                out=held["c", x][:],
                lhsT=c_code[g][:, col].bitcast(E4M3),
                lhsT_scale=c_scale[g][:, col],
                rhs=l_code[g][:].bitcast(E5M2),
                rhs_scale=l_scale[g][:],
                start=(g == 0),
                stop=(g == GY - 1),
            )

        def exp_c(x, j0=0, j1=4):
            b = slice(P * j0, P * j1)
            nc.scalar.activation(
                out=e_x[x][:, b], in_=held["c", x][:, b], func=ACT.Exp, scale=-1.0, bias=score_cols[:, x : x + 1]
            )
            if j1 == 4:
                give_back(("c", x))

        def turn_e(x, j0=0, j1=4):
            tp = new_bank(("e", x, j0), [P, j1 - j0, P])
            for j in range(j0, j1):
                nc.tensor.transpose(tp[:, j - j0, :], e_x[x][:, P * j : P * j + P], ident[:])

        def anchor_mul(x):
            half = P * (x % 2)
            nc.vector.tensor_tensor(
                out=o_sb[x // 2][:, :, half : half + P], in0=held["e", x, 0][:], in1=anc[:, :, P * x : P * x + P], op=MULT
            )
            give_back(("e", x, 0))

        def store(i):
            nc.sync.dma_start(out=out_v[:, :, 256 * i : 256 * i + 256], in_=o_sb[i][:])

        def anchor_mul_store(x, j0, j1):
            cols = slice(P * x, P * x + P)
            half = o_half[x - 6][j0 // 2]
            nc.vector.tensor_tensor(out=half[:], in0=held["e", x, j0][:], in1=anc[:, j0:j1, cols], op=MULT)
            give_back(("e", x, j0))
            nc.sync.dma_start(out=out_v[:, j0:j1, cols], in_=half[:])

        def scales_in(r):
            nc.sync.dma_start(
                out=ws_raw[r:P:32, :, :].bitcast(I32),
                in_=chan_scales[:, r:16:4, :].bitcast(I32).rearrange("k q y -> q k y"),
            )

        def load_anchor(h):
            nc.sync.dma_start(out=anc[:, :, 512 * h : 512 * h + 512], in_=anchor_v[:, :, 512 * h : 512 * h + 512])

        def permute_vectors(copy):
            copy(
                out=vec_perm[:].rearrange("p (t a e) -> p t a e", t=4, e=4),
                in_=vec_rows[:].rearrange("p (a t e) -> p t a e", t=4, e=4),
            )

        def turn_vectors():
            vec_t = new_bank("vec", [P, 5, P], BF16)
            for t in range(4):
                nc.tensor.transpose(vec_t[:, t, :], vec_perm[:, P * t : P * t + P], ident_bf[:])
            nc.tensor.transpose(vec_t[:, 4, :], vec_rows[:, 0:P], ident_bf[:])

        def copy_score(copy):
            copy(out=score_cols[:], in_=held["vec"][:, 4, 4 : 4 + XT])

        vcopy, scopy = nc.vector.tensor_copy, nc.scalar.copy

        with tc.manual_schedule():
            nc.vector.memset(ws_raw[:].rearrange("p k y -> p (k y)").bitcast(I32), 0)
            nc.vector.memset(warm[:], 1.0)
            nc.vector.memset(vec_rows[:], 0.0)
            make_identity(nc, ident[:])
            load_prior(0, 2, 4)
            load_prior(0, 0, 2)
            for r in range(4):
                scales_in(r)
            load_prior(1, 0, 2)
            load_prior(1, 2, 4)
            load_w(0)
            load_c(0, 0, 512)
            load_w(1)
            load_c(0, 512, 1024)
            load_c(1, 0, 1024)
            load_c(2, 0, 1024)
            load_anchor(0)
            load_anchor(1)
            nc.gpsimd.dma_start(out=vec_rows[0:GY, :], in_=beta.rearrange("(g n) -> g n", g=GY))
            nc.gpsimd.dma_start(out=vec_rows[4 : 4 + XT, 0:P], in_=score.rearrange("(r m) -> r m", m=P))
            make_identity(nc, ident_bf[:])
            nc.scalar.activation(out=warm[:, 1:2], in_=warm[:, 0:1], func=ACT.Ln)
            turn_prior(0, 1)
            group_c_beside(1, 512, 768, 0)
            turn_prior(0, 0)
            copy_prior(0, 1, vcopy)
            quant_prior(0, 256, 512)
            turn_prior(1, 0)
            turn_prior(1, 1)
            permute_ws()
            copy_prior(0, 0, scopy)
            quant_prior(0, 0, 256)
            copy_prior(1, 1, scopy)
            permute_w(0)
            quant_prior(1, 256, 512)
            mm1(0, 0)
            mm1(1, 0)
            group_c_beside(1, 256, 512, 1)
            copy_prior(1, 0, scopy)
            quant_prior(1, 0, 256)
            group_c(0, 256, 512, scopy)
            mm1(0, 1)
            mm1(1, 1)
            group_c(0, 0, 256, vcopy)
            permute_w(1)
            quant_c(0, 0, 512)
            log_o(0)
            log_o(1)
            mm1(3, 0)
            mm1(3, 1)
            group_c(0, 512, 768, vcopy)
            log_o(3)
            mm1(2, 0)
            mm1(2, 1)
            mm1(4, 0)
            mm1(7, 0)
            mm1(7, 1)
            permute_vectors(scopy)
            turn_vectors()
            log_o(2)
            mm1(4, 1)
            mm1(6, 0)
            mm1(6, 1)
            mm1(5, 0)
            group_c(0, 768, 1024, vcopy)
            quant_c(0, 512, 768)
            log_o(7)
            log_o(4)
            mm1(5, 1)
            mm1(11, 0)
            mm1(10, 0)
            mm1(10, 1)
            mm1(11, 1)
            log_o(6)
            quant_c(0, 768, 1024)
            beta_mul(0)
            mm1(8, 0)
            log_o(5)
            beta_mul(1)
            mm1(8, 1)
            group_c(1, 0, 256, scopy)
            mm1(9, 0)
            mm1(9, 1)
            quant_l(0)
            mm2(3, 0)
            quant_c(1, 0, 512)
            log_o(8)
            mm2(5, 0)
            mm2(1, 0)
            mm2(2, 0)
            log_o(9)
            quant_l(1)
            log_o(11)
            group_c_beside(2, 0, 256, 2)
            log_o(10)
            mm2(6, 0)
            mm2(3, 1)
            mm2(2, 1)
            beta_mul(2)
            mm2(0, 0)
            mm2(0, 1)
            mm2(7, 0)
            nc.scalar.activation(out=warm[:, 1:2], in_=warm[:, 0:1], func=ACT.Exp)
            quant_c(1, 512, 768)
            group_c(2, 256, 512, scopy)
            quant_l(2)
            group_c(2, 512, 768, scopy)
            quant_c(2, 512, 768)
            mm2(4, 0)
            copy_score(vcopy)
            mm2(4, 1)
            quant_c(2, 0, 512)
            mm2(5, 1)
            group_c(1, 768, 1024, vcopy)
            mm2(1, 1)
            mm2(5, 2)
            mm2(4, 2)
            mm2(3, 2)
            group_c(2, 768, 1024, scopy)
            mm2(2, 2)
            quant_c(2, 768, 1024)
            quant_c(1, 768, 1024)
            exp_c(5)
            mm2(1, 2)
            turn_e(5)
            exp_c(4)
            turn_e(4)
            exp_c(3)
            mm2(0, 2)
            anchor_mul(5)
            exp_c(2)
            anchor_mul(4)
            store(2)
            turn_e(3)
            exp_c(1)
            anchor_mul(3)
            turn_e(2)
            exp_c(0)
            mm2(6, 1)
            anchor_mul(2)
            store(1)
            turn_e(1)
            turn_e(0)
            mm2(6, 2)
            mm2(7, 1)
            exp_c(6, 0, 2)
            anchor_mul(1)
            exp_c(6, 2, 4)
            mm2(7, 2)
            exp_c(7, 0, 2)
            anchor_mul(0)
            store(0)
            exp_c(7, 2, 4)
            turn_e(6, 0, 2)
            anchor_mul_store(6, 0, 2)
            turn_e(6, 2, 4)
            anchor_mul_store(6, 2, 4)
            turn_e(7, 0, 2)
            anchor_mul_store(7, 0, 2)
            turn_e(7, 2, 4)
            anchor_mul_store(7, 2, 4)
